import numpy as np, ml_dtypes
CORES = [24,25,26,27,28,29,30,31]
N = 8
BF = ml_dtypes.bfloat16
S, R, B, CAP = 512, 128, 8, 192
L, IT, I = 2, 8, 16
D, TOP, F = 2, 2, 1
def where_to(rep):
    i = np.arange(N * S); first = np.maximum.accumulate(np.where(rep == 0, i, 0)); rec = np.add.accumulate((rep == 0).astype(np.int64)) - 1
    kth = np.add.accumulate((rep == 1).astype(np.int64)); head = np.maximum.accumulate(np.where(rep < 2, i, 0))
    return rec, kth - kth[first], i - head
def count(rec):
    return np.bincount(np.arange(N * S) // S * N + rec // B % N, minlength=N * N)
def parts(rng, lens, total):
    diff = int(total - np.sum(lens)); room = I - lens if diff > 0 else lens - 1
    k = np.bincount(rng.permutation(np.repeat(np.arange(len(lens)), room))[:abs(diff)], minlength=len(lens))
    return lens + (k if diff > 0 else -k)
def rich(rng, n, total):
    return parts(rng, np.where(rng.random(n) * ((I - 1) * n) < 2 * (total - n), rng.integers(1, I + 1, n), 1), total)
def levels(rng, lens):
    if count(np.repeat(np.arange(len(lens)), lens)).max() > CAP:
        lens = np.diff(np.arange(N * R + 1) * (N * S) // (N * R))
    rep = np.full(N * S, TOP, np.int32); rep[np.add.accumulate(lens) - lens] = 0
    if L > 1:
        u = rng.random(N * S).tolist(); i = 0
        for n in lens.tolist():
            k = c = 1
            for j in range(1, n):
                if c == IT or (k < L and n - j <= (L - k) * IT and u[i + j] < 0.35):
                    rep[i + j] = 1; k += 1; c = 1
                else: c += 1
            i += n
    return rep
def values(rng):
    return rng.integers(0, 1 << 20, (N, 8, S)).astype(np.int32)
def make(rng, cols, p):
    rl = np.ascontiguousarray(np.stack([levels(rng, c) for c in cols]).reshape(8, N, S).transpose(1, 0, 2))
    dl = np.where(rng.random((N, 8, S)) < p, D, rng.integers(0, D, (N, 8, S))).astype(np.int32)
    return {"rl": rl, "dl": dl, "val": values(rng)}
def setup_inputs(rng):
    cols = [rich(rng, int(rng.integers(N * R * 3 // 4, N * R + 1)), N * S) for g in range(8)]
    return make(rng, cols, rng.integers(4, 16, (N, 8, 1)) * 0.0625)
def setup_inputs_full(rng):
    cols = []; mix = rng.permutation(8).tolist(); odd = mix[:4]; home = mix[4]; m = R // N
    for g in range(8):
        if g in odd: cols.append(rich(rng, N * R, N * S)); continue
        c = []
        for q in range(N):
            d = q if g == home else (q + 1 + g % (N - 1)) % N; own = np.arange(R) // B % N == d; v = np.ones(R, np.int64)
            v[own] = parts(rng, v[own], CAP); v[~own] = parts(rng, v[~own], S - CAP); c.append(v)
        cols.append(np.concatenate(c))
    return make(rng, cols, rng.choice(np.array([0.5, 1.0]), (N, 8, 1)))
def setup_inputs_edges(rng):
    cols = []
    for g in range(8):
        a = rng.integers(0, I + 1, N - 1); c = []; at = 0
        if g < 4: a[:] = (0, I, 1, I - 1)[g]
        for q in range(1, N + 1):
            end = q * S - int(a[q - 1]) if q < N else N * S; seg = end - at
            c.append(rich(rng, max(-(-seg // I), seg * R * int(rng.integers(12, 17)) // (16 * S)), seg))
            if q < N: c.append(np.array([I])); at = end + I
        cols.append(np.concatenate(c))
    return make(rng, cols, rng.integers(0, 3, (N, 8, 1)) * 0.5)
def setup_inputs_few(rng):
    cols = []
    for g in range(8):
        h = int(rng.integers(1, I + 1)) if g else I; k = (N * S - h) // I; t = N * S - h - k * I
        cols.append(np.array([h] + [I] * k + ([t] if t else [])))
    p = rng.integers(8, 17, (N, 8, 1)) * 0.0625; p[:, rng.integers(0, 8)] = 0
    return make(rng, cols, p)
def setup_inputs_spread(rng):
    cols = [rich(rng, int(rng.integers(N * S // I, N * R + 1)), N * S) for g in range(8)]
    d = make(rng, cols, rng.integers(1, 16, (N, 8, 1)) * 0.0625)
    v = d["val"] >> rng.integers(0, 21, (N, 8, S)); d["val"] = np.where(rng.random((N, 8, S)) < 0.0625, (1 << 20) - 1, v).astype(np.int32)
    return d
def check_inputs(d):
    rl, dl, val = d["rl"], d["dl"], d["val"]; bad = []
    if not (((rl >= 0) & (rl <= TOP)).all() and ((dl >= 0) & (dl <= D)).all()): bad.append("levels")
    if not (rl[0, :, 0] == 0).all(): bad.append("first")
    if not (((val >= 0) & (val < 1 << 20)).all()): bad.append("values")
    if bad: return bad
    for g in range(8):
        rec, lst, item = where_to(rl[:, g].reshape(-1))
        if rec[-1] >= N * R: bad.append("records")
        if lst.max() >= L or item.max() >= IT: bad.append("items")
        if count(rec).max() > CAP: bad.append("pairs")
    return sorted(set(bad))
def reference(rl, dl, val):
    y = np.full((N, 8, F, R * I), -2, np.float32); x = val.reshape(N, 8, F, S); q = np.arange(N * S) // S
    for g in range(8):
        rec, lst, item = where_to(rl[:, g].reshape(-1)); lev = dl[:, g].reshape(-1)
        has = (dl[:, g] == D).astype(np.int64); v = (np.add.accumulate(has, axis=1) - has).reshape(-1)
        e = np.where((lev == D)[:, None], x[q, g, :, v].astype(np.float32), (lev - D)[:, None])
        y[rec // B % N, g, :, (rec // (B * N) * B + rec % B) * I + lst * IT + item] = e
    return {"y": y.reshape(N, 8 * F, R * I).astype(np.float32)}

@@ -1,0 +1,310 @@
+from concourse.bass import DstId, RemoteDMATransfer
+from concourse.mybir import dt, AluOpType, AxisListType, ActivationFunctionType
+
+SLOTS = 72
+NF = 8 * SLOTS
+NEG = -4194304.0
+MAGIC = 805306368.0
+WIN = 1696
+
+_SBUF = {
+    "int32": "mi 128 mb 128 pi 16 mki 128 raw 64 v 520",
+    "bfloat16": "m1 128 ml1 128 m5 128 m70 128 m71 128 mk 128 r16 2 c1 32 zo 34 ho 32 sz 34 sh 34",
+    "uint16": "codel 32 voffl 32 slotl 34 gl 36 prm 8 elist 4 lst 16",
+    "float32": "pf 16 cols 16 cwin 96 zr 128 tf 64 of 64 rl2 32 ct 32 co 32 nz 34 nh 32 dd 32 s3 32 jc 34 nj 34 "
+               "slf 34 vf 32 oh 512 aa 512 bb 512 ohl 16 el1 16 sc 528 win %d exs 4 ex 36 kc 16 cm 16 cs1 16 cr 1 "
+               "xj 8 x1 4 y1 4 b1 4 ff 72 fd 36 fe 36 cst 36 fr %d land %d ti 64 tq 64 tq1 64 k72 64 bsi 16 bs 16 "
+               "pmi 8 xa 8 ba 8 d8 8 dl8 8 te 64 de 64 ge 64 eq 64 pq 128 cum 132 dif 16 off 16 sec 128 ym 128 "
+               "zt 128 zf0 64 zf1 64" % (WIN, NF, NF + 8),
+}
+SCRATCH = {}
+for _d, _s in _SBUF.items():
+    _s = _s.split()
+    for _n, _w in zip(_s[0::2], _s[1::2]):
+        SCRATCH[_n] = ("sbuf", [128, int(_w)], _d)
+for _n in ("pa", "pb", "pc", "pd"):
+    SCRATCH[_n] = ("psum", [128, 512], "float32")
+SEMAPHORES = ["cv", "cs", "cp", "cg", "ldr", "ldv", "exa", "exl", "ma", "ml", "st"]
+
+
+def rank_program(g, core, T, topo):
+    q = T.rank_of(core)
+    if q is None:
+        return
+    A, ACT = AluOpType, ActivationFunctionType
+    V, S, P = g.vector, g.scalar, g.tensor
+    queues = {"v": V, "s": S, "p": P, "g": g, "y": g.sync}
+    cnt = {k: 0 for k in queues}
+    known = {k: {} for k in queues}
+
+    def use(k, *toks):
+        for sem, val in toks:
+            if known[k].get(sem, 0) < val:
+                queues[k].wait_ge(T.sem[sem], val)
+                known[k][sem] = val
+
+    def done(k, ins):
+        cnt[k] += 1
+        ins.then_inc(T.sem["c" + k], 1)
+        return ("c" + k, cnt[k])
+
+    def ts(out, in0, s1, op0, s2=None, op1=None, w=()):
+        use("v", *w)
+        if op1 is None:
+            return done("v", V.tensor_scalar(out, in0, s1, None, op0))
+        return done("v", V.tensor_scalar(out, in0, s1, s2, op0, op1))
+
+    def tt(out, a, b, op, w=()):
+        use("v", *w)
+        return done("v", V.tensor_tensor(out, a, b, op))
+
+    def cp(out, in_, w=()):
+        use("v", *w)
+        return done("v", V.tensor_copy(out, in_))
+
+    def ms(ap, c, w=()):
+        use("v", *w)
+        return done("v", V.memset(ap, c))
+
+    def tr(out, in_, w=()):
+        use("v", *w)
+        return done("v", V.transpose(out, in_))
+
+    def scan(out, d0, d1, init, op0, op1, w=()):
+        use("v", *w)
+        return done("v", V.tensor_tensor_scan(out, d0, d1, init, op0, op1))
+
+    def act(out, in_, func=None, bias=0.0, scale=1.0, w=(), acc=None):
+        use("s", *w)
+        f = ACT.Identity if func is None else func
+        if acc is not None:
+            return done("s", S.activation(out, in_, f, bias=bias, scale=scale, accum_out=acc))
+        return done("s", S.activation(out, in_, f, bias=bias, scale=scale))
+
+    def mm(out, lhsT, rhs, start, stop, w=()):
+        use("p", *w)
+        return done("p", P.matmul(out, lhsT, rhs, start, stop))
+
+    def iota(out, pattern, base, mult, flag=True):
+        if not flag:
+            return done("g", g.iota(out, pattern, base, mult))
+        return done("g", g.iota(out, pattern, base, mult, allow_small_or_imprecise_dtypes=True))
+
+    LDR, LDV = ("ldr", 64), ("ldv", 256)
+    g.sync.dma_start(T.raw[:, 0:16], T.rl[0::2, :]).then_inc(T.sem.ldr, 16)
+    S.dma_start(T.raw[:, 16:32], T.rl[1::2, :]).then_inc(T.sem.ldr, 16)
+    g.sync.dma_start(T.raw[:, 32:48], T.dl[0::2, :]).then_inc(T.sem.ldr, 16)
+    S.dma_start(T.raw[:, 48:64], T.dl[1::2, :]).then_inc(T.sem.ldr, 16)
+    for w in range(16):
+        qq = S if w % 3 == 2 else g.sync
+        qq.dma_start(T.v[w::16, 0:512], T.val[:, :]).then_inc(T.sem.ldv, 16)
+
+    t_pi = iota(T.pi[:, 0:1], [[0, 1]], 0, 1, False)
+    t_mi = iota(T.mi[:, :], [[1, 128]], 0, 0, False)
+    i_jc = iota(T.jc[:, 0:33], [[16, 33]], 577, 0)
+    i_kc = iota(T.kc[:, :], [[-2, 16]], -2, 0)
+    i_ff = iota(T.ff[:, :], [[8, 8], [64, 9]], 32, 0)
+
+    ms(T.r16[0:1, 0:2], 16.0)
+    ms(T.zr[:, :], 0.0)
+    ms(T.sz[:, 0:1], 0.0)
+    ms(T.sh[:, 0:1], 0.0)
+    m_exs = ms(T.exs[:, :], 0.0)
+    p0 = T.pi[:, 0:1]
+    ts(T.pi[:, 1:2], p0, 15, A.bitwise_and, w=[t_pi])
+    ts(T.pi[:, 2:3], p0, 4, A.logical_shift_right)
+    ts(T.pi[:, 3:4], p0, 5, A.logical_shift_right)
+    ts(T.pi[:, 4:5], p0, 31, A.bitwise_and)
+    ts(T.pi[:, 5:6], p0, 3, A.logical_shift_right, 1, A.bitwise_and)
+    ts(T.pi[:, 6:7], p0, 7, A.bitwise_and)
+    ts(T.pi[:, 7:8], p0, 1, A.logical_shift_right, 7, A.bitwise_and)
+    t = ts(T.pi[:, 8:9], p0, 1, A.bitwise_and)
+    t_mb = ts(T.mb[:, :], T.mi[:, :], 4, A.logical_shift_right, w=[t_mi])
+    t_mki = ts(T.mki[0:1, :], T.mi[0:1, :], 31, A.bitwise_and)
+    t_pf = cp(T.pf[:, 0:9], T.pi[:, 0:9], w=[t])
+    pf = lambda k: T.pf[:, k:k + 1]
+    col = lambda k: T.cols[:, k:k + 1]
+    ts(col(0), pf(4), 31.0, A.is_equal, w=[t_pf])
+    t_c1 = ts(col(1), pf(4), 31.0, A.not_equal)
+    ts(col(7), pf(6), 2.0, A.mult, pf(5), A.add)
+    ts(col(2), pf(3), 2.0, A.mult, 1.0, A.add)
+    ts(col(3), pf(3), 2.0, A.mult, 2.0, A.add)
+    ts(col(9), pf(6), 0.5, A.add)
+    t_m1 = ts(T.m1[:, :], T.mb[:, :], pf(2), A.is_equal, w=[t_mb])
+    t = ts(col(4), pf(0), 2.0, A.add, col(1), A.mult, w=[t_c1])
+    t_c5 = ts(col(5), col(2), col(0), A.mult, w=[t])
+    t_c6 = ts(col(6), col(3), col(0), A.mult)
+    t_mk = ts(T.mk[0:1, :], T.mki[0:1, :], 0.0, A.is_equal, w=[t_mki])
+    t_m5 = ts(T.m5[:, :], T.mi[:, :], 1.0, A.add, col(4), A.is_equal, w=[t])
+    t_m70 = ts(T.m70[:, :], T.mb[:, :], 1.0, A.add, col(5), A.is_equal, w=[t_c5])
+    t_m71 = ts(T.m71[:, :], T.mb[:, :], 1.0, A.add, col(6), A.is_equal, w=[t_c6])
+    ts(T.cwin[:, 0:32], T.mi[:, 0:32], col(7), A.not_equal, NEG, A.mult)
+    ts(T.cwin[:, 32:64], T.mi[:, 0:32], 2097152.0, A.mult, -2.0, A.add)
+    ts(T.cwin[:, 64:96], T.mi[:, 0:32], 16.0, A.is_lt, NEG, A.mult)
+    ts(T.zo[:, 32:33], pf(1), 0.0, A.is_equal)
+    ts(T.nz[:, 32:33], pf(1), 0.0, A.not_equal)
+    ts(T.jc[:, 0:33], T.jc[:, 0:33], pf(1), A.add, w=[i_jc])
+    ms(T.sc[:, 0:1], -2.0)
+    ms(T.sc[:, 513:528], -2.0)
+    ms(T.v[:, 512:513], -1)
+    ms(T.v[:, 513:520], -2)
+    t_exc = ms(T.ex[:, 0:4], -32.5)
+
+    use("g", t_m1)
+    t_l = done("g", g.affine_select(T.ml1[:, :], T.m1[:, :], [[1, 128]], A.is_ge, 0.0, 0, -1))
+    i_ti = iota(T.ti[:, :], [[1, 4], [512, 2], [0, 8]], 8 * q, 0)
+    i_k72 = iota(T.k72[:, :], [[0, 8], [72, 8]], -576, 0)
+    iota(T.bsi[:, 0:8], [[1, 4], [64, 2]], 8, 0)
+    i_bs = iota(T.bsi[:, 8:16], [[1, 4], [0, 2]], 576, 0)
+    i_pm = iota(T.pmi[:, :], [[16, 2], [32, 4]], 0, 0)
+
+    t_tf = cp(T.tf[:, :], T.raw[:, :], w=[LDR])
+    t_of = tr(T.of[:, :], T.tf[:, :], w=[t_tf])
+    t_rl2 = act(T.rl2[:, :], T.tf[:, 0:32], ACT.Relu, -1.0, 1.0, w=[t_tf])
+    t_zo = act(T.zo[:, 0:32], T.of[:, 0:32], ACT.Relu, 1.0, -1.0, w=[t_of])
+    t_ho = act(T.ho[:, :], T.of[:, 32:64], ACT.Relu, -1.0, 1.0)
+    t_nh = act(T.nh[:, :], T.of[:, 32:64], ACT.Relu, 2.0, -1.0)
+    t_s1 = scan(T.c1[:, :], T.rl2[:, :], T.tf[:, 0:32], 0.0, A.mult, A.add, w=[t_rl2])
+    t_sz = scan(T.sz[:, 1:33], T.zo[:, 0:32], T.zr[:, 0:32], 0.0, A.add, A.add, w=[t_zo])
+    t_sh = scan(T.sh[:, 1:33], T.ho[:, :], T.zr[:, 0:32], 0.0, A.add, A.add, w=[t_ho])
+    mm(T.pa[:, 0:2], T.mk[0:1, :], T.r16[0:1, 0:2], True, False, w=[t_mk])
+    t_pa = mm(T.pa[:, 0:2], T.m5[:, :], T.c1[:, 15:32:16], False, True, w=[t_m5, t_s1])
+    mm(T.pb[:, 1:2], T.m70[:, :], T.c1[:, 15:16], True, False, w=[t_m71])
+    mm(T.pb[:, 1:2], T.m71[:, :], T.c1[:, 31:32], False, True)
+    t_pb = mm(T.pb[:, 0:1], T.m1[:, :], T.sz[:, 32:33], True, True, w=[t_sz])
+    mm(T.pd[:, 0:32], T.m1[:, :], T.sh[:, 0:32], True, False, w=[t_sh])
+    t_pd = mm(T.pd[:, 0:32], T.ml1[:, :], T.ho[:, :], False, True, w=[t_l, t_ho])
+    mm(T.pc[:, 0:33], T.m1[:, :], T.sz[:, 0:33], True, False)
+    t_pc = mm(T.pc[:, 0:33], T.ml1[:, :], T.zo[:, 0:33], False, True, w=[t_zo])
+
+    t_exs = act(T.exs[:, 0:2], T.pb[:, 0:2], w=[t_pb, m_exs])
+    others = [c for c in T.cores if c != core]
+
+    def dst_id(c):
+        rid, pid, _ = topo.addr(c)
+        return DstId(rid=rid, pnc=pid)
+
+    def common(src, dsts):
+        m = topo.mask(src, dsts[0])
+        for c in dsts:
+            m &= topo.mask(src, c)
+        return m
+
+    if q < 7:
+        use("g", t_exs)
+        o = 4 * (q + 1)
+        g.remote_dma_fused([RemoteDMATransfer(dst_ids=[dst_id(c) for c in others],
+                                              dma_engine_mask=common(core, others), remote_sem=T.sem.exa,
+                                              src=T.exs[:, :], dsts=[T.ex[:, o:o + 4] for _ in others])],
+                           local_sem=T.sem.exl)
+    EXA = ("exa", sum(bin(common(c, [d for d in T.cores if d != c])).count("1") for c in T.cores[0:7] if c != core))
+
+    scan(T.ct[:, 0:16], T.rl2[:, 0:16], T.tf[:, 0:16], T.pa[:, 0:1], A.mult, A.add, w=[t_pa])
+    t = scan(T.ct[:, 16:32], T.rl2[:, 16:32], T.tf[:, 16:32], T.pa[:, 1:2], A.mult, A.add)
+    t = tr(T.co[:, :], T.ct[:, :], w=[t])
+    t_code = cp(T.codel[:, :], T.co[:, :], w=[t])
+    t_oh = act(T.oh[:, :], T.cwin[:, 0:32].indirect(T.codel[:, 0:32]), w=[t_code])
+    t_ohl = act(T.ohl[:, :], T.cwin[:, 64:96].indirect(T.codel[:, 0:1]))
+    t_aa = act(T.aa[:, :], T.cwin[:, 32:64].indirect(T.codel[:, 0:32]))
+    t = ts(T.dd[:, :], T.nh[:, :], 0.5, A.is_gt, 512.0, A.mult, w=[t_nh])
+    t = tt(T.s3[:, :], T.dd[:, :], T.nh[:, :], A.add, w=[t])
+    t = tt(T.vf[:, :], T.pd[:, 0:32], T.s3[:, :], A.max, w=[t_pd, t])
+    t_voff = ts(T.voffl[:, :], T.vf[:, :], -1.0, A.add, w=[t])
+    t = ts(T.nz[:, 0:32], T.of[:, 0:32], 1.0, A.min)
+    t = tt(T.nj[:, 0:33], T.nz[:, 0:33], T.jc[:, 0:33], A.mult, w=[t])
+    t = tt(T.slf[:, 0:33], T.pc[:, 0:33], T.nj[:, 0:33], A.add, w=[t_pc, t])
+    t_slot = ts(T.slotl[:, 0:33], T.slf[:, 0:33], 63.0, A.add, w=[t])
+    t_win = ms(T.win[:, 0:640], -2.0)
+
+    t_bb = tt(T.bb[:, :], T.v[:, 0:520].indirect(T.voffl[:, 0:32]), T.oh[:, :], A.add, w=[LDV, t_voff, t_oh])
+    t_el = tt(T.el1[:, :], T.v[:, 0:520].indirect(T.voffl[:, 0:1]), T.ohl[:, :], A.add, w=[t_ohl])
+    t_kc = ts(T.kc[:, :], T.kc[:, :], col(7), A.add, w=[i_kc])
+    t = tt(T.fd[:, :], T.ff[:, 1:72:2], T.ff[:, 0:72:2], A.subtract, w=[i_ff])
+    t = ts(T.fe[:, :], T.fd[:, :], pf(5), A.mult, col(9), A.add, w=[t])
+    t_cst = tt(T.cst[:, :], T.fe[:, :], T.ff[:, 0:72:2], A.add, w=[t])
+    t = scan(T.sc[:, 1:513], T.aa[:, :], T.bb[:, :], -2.0, A.min, A.max, w=[t_bb, t_aa])
+    t_scat = cp(T.win[:, 0:WIN].indirect(T.slotl[:, 0:33]), T.sc[:, :], w=[t, t_slot, t_win])
+
+    t_x = act(T.xj[:, 0:q + 1], T.ex[:, 0:4 * q + 1:4], w=[t_exc] + ([EXA] if q else []), acc=T.x1[:, 0:1])
+    t = act(T.y1[:, 0:1], T.x1[:, 0:1], None, MAGIC, w=[t_x])
+    t_b = act(T.b1[:, 0:1], T.y1[:, 0:1], None, -MAGIC, w=[t])
+    t_fix = t_scat
+    if q:
+        c = T.ex[:, 4 * q + 1:4 * q + 2]
+        t = ts(T.cm[:, :], T.kc[:, :], c, A.not_equal, NEG, A.mult, w=[EXA, t_kc])
+        t = tt(T.cs1[:, :], T.cm[:, :], T.el1[:, :], A.add, w=[t, t_el])
+        use("v", t)
+        t = done("v", V.tensor_reduce(T.cr[:, :], T.cs1[:, :], AxisListType.X, A.max))
+        t_fix = tt(T.win[:, 64:65], T.win[:, 64:65], T.cr[:, :], A.max, w=[t, t_scat])
+    t_gl = ts(T.gl[:, :], T.cst[:, :], T.b1[:, 0:1], A.add, T.x1[:, 0:1], A.subtract, w=[t_b, t_x, t_cst])
+    t_f0 = cp(T.fr[:, 0:288], T.win[:, 0:640].indirect(T.gl[:, 0:18]), w=[t_gl, t_fix])
+    t_f1 = act(T.fr[:, 288:576], T.win[:, 0:640].indirect(T.gl[:, 18:36]), w=[t_gl, t_fix])
+
+    near = [d for d in range(8) if d != q and topo.die(T.cores[d]) == topo.die(core)]
+    far = [d for d in range(8) if d != q and topo.die(T.cores[d]) != topo.die(core)]
+    trs, k = [], 0
+    while near or far:
+        for h, side in enumerate((far, near)):
+            if not side:
+                continue
+            d = side.pop(0)
+            e = topo.engines(core, T.cores[d])
+            trs.append(RemoteDMATransfer(dst_ids=[dst_id(T.cores[d])],
+                                         dma_engine_mask=(1 << e[k + h]) | (1 << e[k + 2 + h]),
+                                         remote_sem=T.sem.ma, src=T.fr[:, SLOTS * d:SLOTS * d + SLOTS],
+                                         dst=T.land[:, SLOTS * q:SLOTS * q + SLOTS]))
+        k += 4
+    use("g", t_f0, t_f1)
+    g.remote_dma_fused(trs, local_sem=T.sem.ml)
+
+    t_own = t_exc
+    if q < 7:
+        t_own = act(T.ex[:, 4 * q + 4:4 * q + 8], T.exs[:, :], w=[t_exs])
+    t_me = act(T.land[:, SLOTS * q:SLOTS * q + SLOTS], T.fr[:, SLOTS * q:SLOTS * q + SLOTS], w=[t_f0, t_f1])
+    ms(T.d8[:, 0:1], 576.0)
+    ms(T.cum[:, 0:1], 0.0)
+    t_ls = ms(T.land[:, NF:NF + 8], -2.0)
+    ts(T.elist[:, :], T.zr[:, 0:4], pf(6), A.add)
+    t_prm = ts(T.prm[:, :], T.pmi[:, :], pf(1), A.add, w=[i_pm])
+    ts(col(10), pf(7), 64.0, A.mult)
+    ts(col(11), pf(7), 8.0, A.mult)
+    ts(col(12), pf(8), 4.0, A.mult)
+    ts(col(13), pf(8), 4.0, A.mult, -32.5, A.add)
+    t = ts(col(14), pf(8), 4.0, A.mult, -31.5, A.add)
+    ts(T.tq[:, :], T.ti[:, :], col(10), A.add, col(13), A.add, w=[i_ti, t])
+    ts(T.tq1[:, :], T.ti[:, :], col(10), A.add, col(14), A.add)
+    ts(T.bs[:, 0:8], T.bsi[:, 0:8], col(11), A.add, col(12), A.add, w=[i_bs])
+    ts(T.bs[:, 8:16], T.bsi[:, 8:16], col(12), A.add)
+    t_xa = scan(T.xa[:, :], T.ex[:, 0:32:4], T.zr[:, 0:8], 0.0, A.add, A.add, w=[EXA, t_own])
+    t = ts(T.ba[:, :], T.xa[:, :], MAGIC, A.add, MAGIC, A.subtract, w=[t_xa])
+    t = tt(T.d8[:, 1:8], T.ba[:, 1:8], T.ba[:, 0:7], A.subtract, w=[t])
+    t_dl8 = ts(T.dl8[:, :], T.d8[:, :], -0.125, A.mult, 72.0, A.add, w=[t])
+    t_de = act(T.de[:, :], T.dl8[:, 0:8].indirect(T.elist[:, 0:4]), w=[t_dl8])
+    t_te = cp(T.te[:, :], T.xa[:, 0:8].indirect(T.elist[:, 0:4]))
+    t_ge = tt(T.ge[:, :], T.tq[:, :], T.te[:, :], A.is_ge, w=[t_te])
+    t_eq = tt(T.eq[:, :], T.tq1[:, :], T.te[:, :], A.is_equal)
+    tt(T.pq[:, 64:128], T.eq[:, :], T.k72[:, :], A.mult, w=[t_eq, i_k72])
+    t = tt(T.pq[:, 0:64], T.ge[:, :], T.de[:, :], A.mult, w=[t_ge, t_de])
+    t = scan(T.cum[:, 1:129], T.pq[:, :], T.zr[:, 0:128], 0.0, A.add, A.add, w=[t])
+    t = tt(T.dif[:, :], T.cum[:, 8:129:8], T.cum[:, 0:128:8], A.subtract, w=[t])
+    t = tt(T.off[:, :], T.dif[:, :], T.bs[:, :], A.add, w=[t])
+    t_lst = ts(T.lst[:, :], T.off[:, :], float(NF + 7), A.min, w=[t])
+
+    MA = ("ma", 14)
+    t_sec = act(T.sec[:, :], T.land[:, 0:NF + 8].indirect(T.lst[:, 8:16]), w=[t_lst, t_ls, t_me, MA])
+    t = tt(T.ym[:, :], T.land[:, 0:NF + 8].indirect(T.lst[:, 0:8]), T.sec[:, :], A.max,
+           w=[MA, t_lst, t_ls, t_me, t_sec])
+    t_zt = tr(T.zt[:, :], T.ym[:, :], w=[t])
+    t_z0 = cp(T.zf0[:, :], T.zt[:, :].indirect(T.prm[:, 0:4]), w=[t_zt, t_prm])
+    t_z1 = act(T.zf1[:, :], T.zt[:, :].indirect(T.prm[:, 4:8]), w=[t_zt])
+    use("y", t_z0)
+    g.sync.dma_start(T.y[0::2, :], T.zf0[:, :]).then_inc(T.sem.st, 16)
+    use("s", t_z1)
+    S.dma_start(T.y[1::2, :], T.zf1[:, :]).then_inc(T.sem.st, 16)
+
+    use("y", ("st", 32))
+    for k in ("v", "s", "p", "g"):
+        use("g", ("c" + k, cnt[k]))
+    if q < 7:
+        use("g", ("exl", bin(common(core, others)).count("1")))
+    use("g", ("ml", 14), EXA)

@@ -8,12 +8,12 @@ MAGIC = 805306368.0
 WIN = 1696
 
 _SBUF = {
-    "int32": "mi 128 mb 128 pi 16 mki 128 raw 64 v 520",
-    "bfloat16": "m1 128 ml1 128 m5 128 m70 128 m71 128 mk 128 r16 2 c1 32 zo 34 ho 32 sz 34 sh 34",
+    "int32": "pi 16 pj 16 raw 64 v 520",
+    "bfloat16": "mi 128 mb 128 m1 128 ml1 128 m5 128 m70 128 m71 128 mki 128 mk 128 r16 2 c1 32 zo 34 ho 32 szh 68",
     "uint16": "codel 32 voffl 32 slotl 34 gl 36 prm 8 elist 4 lst 16",
-    "float32": "pf 16 cols 16 cwin 96 zr 128 tf 64 of 64 rl2 32 ct 32 co 32 nz 34 nh 32 dd 32 s3 32 jc 34 nj 34 "
-               "slf 34 vf 32 oh 512 aa 512 bb 512 ohl 16 el1 16 sc 528 win %d exs 4 ex 36 kc 16 cm 16 cs1 16 cr 1 "
-               "xj 8 x1 4 y1 4 b1 4 ff 72 fd 36 fe 36 cst 36 fr %d land %d ti 64 tq 64 tq1 64 k72 64 bsi 16 bs 16 "
+    "float32": "pf 16 cols 16 cwin 96 ctmp 64 zr 128 tf 64 of 64 rl2 32 ct 32 co 32 nz 34 nh 32 dd 32 s3 32 jc 34 nj 34 "
+               "slf 34 vf 32 oh 512 aa 512 bb 512 ohl 16 el1 16 sc 528 win %d exs 2 ex 36 kc 16 cm 16 cs1 16 "
+               "ff 72 fd 36 fe 36 cst 36 fr %d land %d ti 64 tq 64 tq1 64 k72 64 bsi 16 bs 16 "
                "pmi 8 xa 8 ba 8 d8 8 dl8 8 te 64 de 64 ge 64 eq 64 pq 128 cum 132 dif 16 off 16 sec 128 ym 128 "
                "zt 128 zf0 64 zf1 64" % (WIN, NF, NF + 8),
 }
@@ -24,7 +24,7 @@ for _d, _s in _SBUF.items():
         SCRATCH[_n] = ("sbuf", [128, int(_w)], _d)
 for _n in ("pa", "pb", "pc", "pd"):
     SCRATCH[_n] = ("psum", [128, 512], "float32")
-SEMAPHORES = ["cv", "cs", "cp", "cg", "ldr", "ldv", "exa", "exl", "ma", "ml", "st"]
+SEMAPHORES = ["cv", "cs", "cp", "cg", "ldr", "ldd", "ldv", "exa", "exl", "ma", "ml", "st"]
 
 
 def rank_program(g, core, T, topo):
@@ -74,12 +74,9 @@ def rank_program(g, core, T, topo):
         use("v", *w)
         return done("v", V.tensor_tensor_scan(out, d0, d1, init, op0, op1))
 
-    def act(out, in_, func=None, bias=0.0, scale=1.0, w=(), acc=None):
+    def act(out, in_, func=None, bias=0.0, scale=1.0, w=()):
         use("s", *w)
-        f = ACT.Identity if func is None else func
-        if acc is not None:
-            return done("s", S.activation(out, in_, f, bias=bias, scale=scale, accum_out=acc))
-        return done("s", S.activation(out, in_, f, bias=bias, scale=scale))
+        return done("s", S.activation(out, in_, ACT.Identity if func is None else func, bias=bias, scale=scale))
 
     def mm(out, lhsT, rhs, start, stop, w=()):
         use("p", *w)
@@ -90,94 +87,82 @@ def rank_program(g, core, T, topo):
             return done("g", g.iota(out, pattern, base, mult))
         return done("g", g.iota(out, pattern, base, mult, allow_small_or_imprecise_dtypes=True))
 
-    LDR, LDV = ("ldr", 64), ("ldv", 256)
+    pf = lambda k: T.pf[:, k:k + 1]
+    col = lambda k: T.cols[:, k:k + 1]
+
+    LDR, LDD, LDV = ("ldr", 32), ("ldd", 32), ("ldv", 256)
     g.sync.dma_start(T.raw[:, 0:16], T.rl[0::2, :]).then_inc(T.sem.ldr, 16)
     S.dma_start(T.raw[:, 16:32], T.rl[1::2, :]).then_inc(T.sem.ldr, 16)
-    g.sync.dma_start(T.raw[:, 32:48], T.dl[0::2, :]).then_inc(T.sem.ldr, 16)
-    S.dma_start(T.raw[:, 48:64], T.dl[1::2, :]).then_inc(T.sem.ldr, 16)
+    g.sync.dma_start(T.raw[:, 32:48], T.dl[0::2, :]).then_inc(T.sem.ldd, 16)
+    S.dma_start(T.raw[:, 48:64], T.dl[1::2, :]).then_inc(T.sem.ldd, 16)
     for w in range(16):
-        qq = S if w % 3 == 2 else g.sync
+        qq = S if w % 4 == 2 else g.sync
         qq.dma_start(T.v[w::16, 0:512], T.val[:, :]).then_inc(T.sem.ldv, 16)
 
     t_pi = iota(T.pi[:, 0:1], [[0, 1]], 0, 1, False)
-    t_mi = iota(T.mi[:, :], [[1, 128]], 0, 0, False)
+    i_mb = iota(T.mb[:, :], [[1, 8], [0, 16]], 0, 0)
+    i_mi = iota(T.mi[:, :], [[1, 128]], 0, 0)
+    i_mk = iota(T.mki[0:1, :], [[0, 4], [1, 32]], 0, 0)
     i_jc = iota(T.jc[:, 0:33], [[16, 33]], 577, 0)
-    i_kc = iota(T.kc[:, :], [[-2, 16]], -2, 0)
     i_ff = iota(T.ff[:, :], [[8, 8], [64, 9]], 32, 0)
+    i_kc = iota(T.kc[:, :], [[-2, 16]], -2, 0)
+    i_v = iota(T.v[:, 512:520], [[-1, 8]], -1, 0, False)
 
+    ms(T.zr[:, 0:32], 0.0)
+    ms(T.szh[:, 0:68:34], 0.0)
     ms(T.r16[0:1, 0:2], 16.0)
-    ms(T.zr[:, :], 0.0)
-    ms(T.sz[:, 0:1], 0.0)
-    ms(T.sh[:, 0:1], 0.0)
-    m_exs = ms(T.exs[:, :], 0.0)
     p0 = T.pi[:, 0:1]
-    ts(T.pi[:, 1:2], p0, 15, A.bitwise_and, w=[t_pi])
-    ts(T.pi[:, 2:3], p0, 4, A.logical_shift_right)
-    ts(T.pi[:, 3:4], p0, 5, A.logical_shift_right)
-    ts(T.pi[:, 4:5], p0, 31, A.bitwise_and)
-    ts(T.pi[:, 5:6], p0, 3, A.logical_shift_right, 1, A.bitwise_and)
-    ts(T.pi[:, 6:7], p0, 7, A.bitwise_and)
-    ts(T.pi[:, 7:8], p0, 1, A.logical_shift_right, 7, A.bitwise_and)
-    t = ts(T.pi[:, 8:9], p0, 1, A.bitwise_and)
-    t_mb = ts(T.mb[:, :], T.mi[:, :], 4, A.logical_shift_right, w=[t_mi])
-    t_mki = ts(T.mki[0:1, :], T.mi[0:1, :], 31, A.bitwise_and)
-    t_pf = cp(T.pf[:, 0:9], T.pi[:, 0:9], w=[t])
-    pf = lambda k: T.pf[:, k:k + 1]
-    col = lambda k: T.cols[:, k:k + 1]
-    ts(col(0), pf(4), 31.0, A.is_equal, w=[t_pf])
-    t_c1 = ts(col(1), pf(4), 31.0, A.not_equal)
-    ts(col(7), pf(6), 2.0, A.mult, pf(5), A.add)
-    ts(col(2), pf(3), 2.0, A.mult, 1.0, A.add)
-    ts(col(3), pf(3), 2.0, A.mult, 2.0, A.add)
-    ts(col(9), pf(6), 0.5, A.add)
-    t_m1 = ts(T.m1[:, :], T.mb[:, :], pf(2), A.is_equal, w=[t_mb])
-    t = ts(col(4), pf(0), 2.0, A.add, col(1), A.mult, w=[t_c1])
-    t_c5 = ts(col(5), col(2), col(0), A.mult, w=[t])
-    t_c6 = ts(col(6), col(3), col(0), A.mult)
-    t_mk = ts(T.mk[0:1, :], T.mki[0:1, :], 0.0, A.is_equal, w=[t_mki])
-    t_m5 = ts(T.m5[:, :], T.mi[:, :], 1.0, A.add, col(4), A.is_equal, w=[t])
-    t_m70 = ts(T.m70[:, :], T.mb[:, :], 1.0, A.add, col(5), A.is_equal, w=[t_c5])
-    t_m71 = ts(T.m71[:, :], T.mb[:, :], 1.0, A.add, col(6), A.is_equal, w=[t_c6])
-    ts(T.cwin[:, 0:32], T.mi[:, 0:32], col(7), A.not_equal, NEG, A.mult)
-    ts(T.cwin[:, 32:64], T.mi[:, 0:32], 2097152.0, A.mult, -2.0, A.add)
-    ts(T.cwin[:, 64:96], T.mi[:, 0:32], 16.0, A.is_lt, NEG, A.mult)
-    ts(T.zo[:, 32:33], pf(1), 0.0, A.is_equal)
-    ts(T.nz[:, 32:33], pf(1), 0.0, A.not_equal)
-    ts(T.jc[:, 0:33], T.jc[:, 0:33], pf(1), A.add, w=[i_jc])
+    ts(T.pi[:, 1:2], p0, 31, A.bitwise_and, w=[t_pi])
+    ts(T.pi[:, 2:3], p0, 15, A.bitwise_and)
+    ts(T.pi[:, 3:4], p0, 3, A.logical_shift_right, 1, A.bitwise_and)
+    ts(T.pi[:, 4:5], p0, 7, A.bitwise_and)
+    t = ts(T.pi[:, 5:6], p0, 4, A.logical_shift_right)
+    t_pf = cp(T.pf[:, 0:6], T.pi[:, 0:6], w=[t])
+    ts(col(0), pf(1), 31.0, A.is_equal, w=[t_pf])
+    ts(col(1), pf(1), 31.0, A.not_equal)
+    ts(col(2), pf(5), -1.0, A.add)
+    t = ts(col(3), pf(0), 1.0, A.add)
+    t_m1 = ts(T.m1[:, :], T.mb[:, :], pf(5), A.is_equal, w=[i_mb])
+    ts(T.m70[:, :], T.mb[:, :], col(2), A.is_equal, col(0), A.mult, w=[t])
+    ts(T.m71[:, :], T.mb[:, :], pf(5), A.is_equal, col(0), A.mult)
+    ts(T.m5[:, :], T.mi[:, :], col(3), A.is_equal, col(1), A.mult, w=[i_mi])
+    t_exc = ms(T.ex[:, 0:1], -32.5)
+    t_mk = ts(T.mk[0:1, :], T.mki[0:1, :], 0.0, A.is_equal, w=[i_mk])
+    ts(T.zo[:, 32:33], pf(2), 0.0, A.is_equal)
+    ts(T.nz[:, 32:33], pf(2), 0.0, A.not_equal)
     ms(T.sc[:, 0:1], -2.0)
     ms(T.sc[:, 513:528], -2.0)
-    ms(T.v[:, 512:513], -1)
-    ms(T.v[:, 513:520], -2)
-    t_exc = ms(T.ex[:, 0:4], -32.5)
+    t_win0 = ms(T.win[:, 512:640], -2.0)
+
+    t = act(col(7), pf(4), None, pf(3), 2.0, w=[t_pf])
+    t_c9 = act(col(9), pf(4), None, 0.5)
+    act(T.cwin[:, 32:64], T.mi[:, 0:32], None, -2.0, 2097152.0, w=[i_mi])
+    t_ct = act(T.ctmp[:, 32:64], T.mi[:, 0:32], ACT.Relu, 16.0, -1.0)
+    t_c7 = act(T.ctmp[:, 0:32], T.mi[:, 0:32], ACT.Abs, col(7), -1.0, w=[t])
+    t_jc = act(T.jc[:, 0:33], T.jc[:, 0:33], None, pf(2), w=[i_jc])
+    act(T.cwin[:, 64:96], T.ctmp[:, 32:64], None, 0.0, NEG, w=[t_ct])
+    t_cw = act(T.cwin[:, 0:32], T.ctmp[:, 0:32], None, 0.0, NEG, w=[t_c7])
+    t_kc = act(T.kc[:, :], T.kc[:, :], None, col(7), w=[i_kc])
 
     use("g", t_m1)
     t_l = done("g", g.affine_select(T.ml1[:, :], T.m1[:, :], [[1, 128]], A.is_ge, 0.0, 0, -1))
-    i_ti = iota(T.ti[:, :], [[1, 4], [512, 2], [0, 8]], 8 * q, 0)
-    i_k72 = iota(T.k72[:, :], [[0, 8], [72, 8]], -576, 0)
-    iota(T.bsi[:, 0:8], [[1, 4], [64, 2]], 8, 0)
-    i_bs = iota(T.bsi[:, 8:16], [[1, 4], [0, 2]], 576, 0)
-    i_pm = iota(T.pmi[:, :], [[16, 2], [32, 4]], 0, 0)
 
-    t_tf = cp(T.tf[:, :], T.raw[:, :], w=[LDR])
-    t_of = tr(T.of[:, :], T.tf[:, :], w=[t_tf])
-    t_rl2 = act(T.rl2[:, :], T.tf[:, 0:32], ACT.Relu, -1.0, 1.0, w=[t_tf])
-    t_zo = act(T.zo[:, 0:32], T.of[:, 0:32], ACT.Relu, 1.0, -1.0, w=[t_of])
-    t_ho = act(T.ho[:, :], T.of[:, 32:64], ACT.Relu, -1.0, 1.0)
-    t_nh = act(T.nh[:, :], T.of[:, 32:64], ACT.Relu, 2.0, -1.0)
+    t_tf = cp(T.tf[:, 0:32], T.raw[:, 0:32], w=[LDR])
+    t_rl2 = ts(T.rl2[:, :], T.raw[:, 0:32], 2.0, A.is_equal)
+    t_of = tr(T.of[:, 0:32], T.tf[:, 0:32], w=[t_tf])
     t_s1 = scan(T.c1[:, :], T.rl2[:, :], T.tf[:, 0:32], 0.0, A.mult, A.add, w=[t_rl2])
-    t_sz = scan(T.sz[:, 1:33], T.zo[:, 0:32], T.zr[:, 0:32], 0.0, A.add, A.add, w=[t_zo])
-    t_sh = scan(T.sh[:, 1:33], T.ho[:, :], T.zr[:, 0:32], 0.0, A.add, A.add, w=[t_ho])
+    t_zo = ts(T.zo[:, 0:32], T.of[:, 0:32], 0.0, A.is_equal, w=[t_of])
+    t_nz = ts(T.nz[:, 0:32], T.of[:, 0:32], 1.0, A.min)
+    t_sz = scan(T.szh[:, 1:33], T.zo[:, 0:32], T.zr[:, 0:32], 0.0, A.add, A.add, w=[t_zo])
     mm(T.pa[:, 0:2], T.mk[0:1, :], T.r16[0:1, 0:2], True, False, w=[t_mk])
-    t_pa = mm(T.pa[:, 0:2], T.m5[:, :], T.c1[:, 15:32:16], False, True, w=[t_m5, t_s1])
-    mm(T.pb[:, 1:2], T.m70[:, :], T.c1[:, 15:16], True, False, w=[t_m71])
+    t_pa = mm(T.pa[:, 0:2], T.m5[:, :], T.c1[:, 15:32:16], False, True, w=[t_s1])
+    mm(T.pb[:, 1:2], T.m70[:, :], T.c1[:, 15:16], True, False)
     mm(T.pb[:, 1:2], T.m71[:, :], T.c1[:, 31:32], False, True)
-    t_pb = mm(T.pb[:, 0:1], T.m1[:, :], T.sz[:, 32:33], True, True, w=[t_sz])
-    mm(T.pd[:, 0:32], T.m1[:, :], T.sh[:, 0:32], True, False, w=[t_sh])
-    t_pd = mm(T.pd[:, 0:32], T.ml1[:, :], T.ho[:, :], False, True, w=[t_l, t_ho])
-    mm(T.pc[:, 0:33], T.m1[:, :], T.sz[:, 0:33], True, False)
-    t_pc = mm(T.pc[:, 0:33], T.ml1[:, :], T.zo[:, 0:33], False, True, w=[t_zo])
+    t_pb = mm(T.pb[:, 0:1], T.m1[:, :], T.szh[:, 32:33], True, True, w=[t_sz])
+    mm(T.pc[:, 0:33], T.m1[:, :], T.szh[:, 0:33], True, False)
+    t_pc = mm(T.pc[:, 0:33], T.ml1[:, :], T.zo[:, 0:33], False, True, w=[t_zo, t_l])
 
-    t_exs = act(T.exs[:, 0:2], T.pb[:, 0:2], w=[t_pb, m_exs])
+    t_exs = act(T.exs[:, :], T.pb[:, 0:2], w=[t_pb])
     others = [c for c in T.cores if c != core]
 
     def dst_id(c):
@@ -195,48 +180,62 @@ def rank_program(g, core, T, topo):
         o = 4 * (q + 1)
         g.remote_dma_fused([RemoteDMATransfer(dst_ids=[dst_id(c) for c in others],
                                               dma_engine_mask=common(core, others), remote_sem=T.sem.exa,
-                                              src=T.exs[:, :], dsts=[T.ex[:, o:o + 4] for _ in others])],
+                                              src=T.exs[:, :], dsts=[T.ex[:, o:o + 2] for _ in others])],
                            local_sem=T.sem.exl)
     EXA = ("exa", sum(bin(common(c, [d for d in T.cores if d != c])).count("1") for c in T.cores[0:7] if c != core))
+    i_ti = iota(T.ti[:, :], [[1, 4], [512, 2], [0, 8]], 8 * q, 0)
+    i_k72 = iota(T.k72[:, :], [[0, 8], [72, 8]], -576, 0)
+    iota(T.bsi[:, 0:8], [[1, 4], [64, 2]], 8, 0)
+    i_bs = iota(T.bsi[:, 8:16], [[1, 4], [0, 2]], 576, 0)
+    i_pm = iota(T.pmi[:, :], [[16, 2], [32, 4]], 0, 0)
 
     scan(T.ct[:, 0:16], T.rl2[:, 0:16], T.tf[:, 0:16], T.pa[:, 0:1], A.mult, A.add, w=[t_pa])
     t = scan(T.ct[:, 16:32], T.rl2[:, 16:32], T.tf[:, 16:32], T.pa[:, 1:2], A.mult, A.add)
+    t_nj = tt(T.nj[:, 0:33], T.nz[:, 0:33], T.jc[:, 0:33], A.mult, w=[t_nz, t_jc])
     t = tr(T.co[:, :], T.ct[:, :], w=[t])
+    t_fd = tt(T.fd[:, :], T.ff[:, 1:72:2], T.ff[:, 0:72:2], A.subtract, w=[i_ff])
     t_code = cp(T.codel[:, :], T.co[:, :], w=[t])
-    t_oh = act(T.oh[:, :], T.cwin[:, 0:32].indirect(T.codel[:, 0:32]), w=[t_code])
+    t_oh = act(T.oh[:, :], T.cwin[:, 0:32].indirect(T.codel[:, 0:32]), w=[t_code, t_cw])
     t_ohl = act(T.ohl[:, :], T.cwin[:, 64:96].indirect(T.codel[:, 0:1]))
     t_aa = act(T.aa[:, :], T.cwin[:, 32:64].indirect(T.codel[:, 0:32]))
-    t = ts(T.dd[:, :], T.nh[:, :], 0.5, A.is_gt, 512.0, A.mult, w=[t_nh])
-    t = tt(T.s3[:, :], T.dd[:, :], T.nh[:, :], A.add, w=[t])
-    t = tt(T.vf[:, :], T.pd[:, 0:32], T.s3[:, :], A.max, w=[t_pd, t])
+    t_win = act(T.win[:, 0:512], T.oh[:, :], None, -2.0, 0.0, w=[t_oh])
+    t_own = t_exc
+    if q < 7:
+        t_own = act(T.ex[:, 4 * q + 4:4 * q + 6], T.exs[:, :], w=[t_exs])
+    t_tfd = cp(T.tf[:, 32:64], T.raw[:, 32:64], w=[LDD])
+    t_slf = tt(T.slf[:, 0:33], T.pc[:, 0:33], T.nj[:, 0:33], A.add, w=[t_pc, t_nj])
+    t_ofd = tr(T.of[:, 32:64], T.tf[:, 32:64], w=[t_tfd])
+    t_slot = ts(T.slotl[:, 0:33], T.slf[:, 0:33], 63.0, A.add, w=[t_slf])
+    t_ho = ts(T.ho[:, :], T.of[:, 32:64], 2.0, A.is_equal, w=[t_ofd])
+    ts(T.nh[:, :], T.of[:, 32:64], -1.0, A.mult, 2.0, A.add)
+    t_sh = scan(T.szh[:, 35:67], T.ho[:, :], T.zr[:, 0:32], 0.0, A.add, A.add, w=[t_ho])
+    mm(T.pd[:, 0:32], T.ml1[:, :], T.ho[:, :], True, False, w=[t_ho])
+    t_pd = mm(T.pd[:, 0:32], T.m1[:, :], T.szh[:, 34:66], False, True, w=[t_sh])
+    t_dd = ts(T.dd[:, :], T.of[:, 32:64], 2.0, A.is_lt, 512.0, A.mult)
+    ts(T.fe[:, :], T.fd[:, :], pf(3), A.mult, col(9), A.add, w=[t_fd, t_c9])
+    t_s3 = tt(T.s3[:, :], T.dd[:, :], T.nh[:, :], A.add, w=[t_dd])
+    t = tt(T.vf[:, :], T.pd[:, 0:32], T.s3[:, :], A.max, w=[t_pd, t_s3])
+    t_cst = tt(T.cst[:, :], T.fe[:, :], T.ff[:, 0:72:2], A.add)
     t_voff = ts(T.voffl[:, :], T.vf[:, :], -1.0, A.add, w=[t])
-    t = ts(T.nz[:, 0:32], T.of[:, 0:32], 1.0, A.min)
-    t = tt(T.nj[:, 0:33], T.nz[:, 0:33], T.jc[:, 0:33], A.mult, w=[t])
-    t = tt(T.slf[:, 0:33], T.pc[:, 0:33], T.nj[:, 0:33], A.add, w=[t_pc, t])
-    t_slot = ts(T.slotl[:, 0:33], T.slf[:, 0:33], 63.0, A.add, w=[t])
-    t_win = ms(T.win[:, 0:640], -2.0)
 
-    t_bb = tt(T.bb[:, :], T.v[:, 0:520].indirect(T.voffl[:, 0:32]), T.oh[:, :], A.add, w=[LDV, t_voff, t_oh])
-    t_el = tt(T.el1[:, :], T.v[:, 0:520].indirect(T.voffl[:, 0:1]), T.ohl[:, :], A.add, w=[t_ohl])
-    t_kc = ts(T.kc[:, :], T.kc[:, :], col(7), A.add, w=[i_kc])
-    t = tt(T.fd[:, :], T.ff[:, 1:72:2], T.ff[:, 0:72:2], A.subtract, w=[i_ff])
-    t = ts(T.fe[:, :], T.fd[:, :], pf(5), A.mult, col(9), A.add, w=[t])
-    t_cst = tt(T.cst[:, :], T.fe[:, :], T.ff[:, 0:72:2], A.add, w=[t])
+    t_bb = tt(T.bb[:, :], T.v[:, 0:520].indirect(T.voffl[:, 0:32]), T.oh[:, :], A.add, w=[LDV, i_v, t_voff, t_oh])
     t = scan(T.sc[:, 1:513], T.aa[:, :], T.bb[:, :], -2.0, A.min, A.max, w=[t_bb, t_aa])
-    t_scat = cp(T.win[:, 0:WIN].indirect(T.slotl[:, 0:33]), T.sc[:, :], w=[t, t_slot, t_win])
+    t_el = tt(T.el1[:, :], T.v[:, 0:520].indirect(T.voffl[:, 0:1]), T.ohl[:, :], A.add, w=[t_ohl])
+    t_scat = cp(T.win[:, 0:WIN].indirect(T.slotl[:, 0:33]), T.sc[:, :], w=[t, t_slot, t_win0, t_win])
 
-    t_x = act(T.xj[:, 0:q + 1], T.ex[:, 0:4 * q + 1:4], w=[t_exc] + ([EXA] if q else []), acc=T.x1[:, 0:1])
-    t = act(T.y1[:, 0:1], T.x1[:, 0:1], None, MAGIC, w=[t_x])
-    t_b = act(T.b1[:, 0:1], T.y1[:, 0:1], None, -MAGIC, w=[t])
+    if q:
+        t_w64 = act(T.cs1[:, 15:16], T.win[:, 64:65], w=[t_scat])
+    t_xa = scan(T.xa[:, :], T.ex[:, 0:32:4], T.zr[:, 0:8], 0.0, A.add, A.add, w=[EXA, t_own])
+    if q:
+        t_cm = ts(T.cm[:, :], T.kc[:, :], T.ex[:, 4 * q + 1:4 * q + 2], A.not_equal, NEG, A.mult, w=[t_kc])
+    t_ba = ts(T.ba[:, :], T.xa[:, :], MAGIC, A.add, MAGIC, A.subtract, w=[t_xa])
+    if q:
+        t_cs1 = tt(T.cs1[:, 0:15], T.cm[:, 0:15], T.el1[:, 0:15], A.add, w=[t_cm, t_el])
+    t_gl = ts(T.gl[:, :], T.cst[:, :], T.ba[:, q:q + 1], A.add, T.xa[:, q:q + 1], A.subtract, w=[t_ba, t_cst])
     t_fix = t_scat
     if q:
-        c = T.ex[:, 4 * q + 1:4 * q + 2]
-        t = ts(T.cm[:, :], T.kc[:, :], c, A.not_equal, NEG, A.mult, w=[EXA, t_kc])
-        t = tt(T.cs1[:, :], T.cm[:, :], T.el1[:, :], A.add, w=[t, t_el])
-        use("v", t)
-        t = done("v", V.tensor_reduce(T.cr[:, :], T.cs1[:, :], AxisListType.X, A.max))
-        t_fix = tt(T.win[:, 64:65], T.win[:, 64:65], T.cr[:, :], A.max, w=[t, t_scat])
-    t_gl = ts(T.gl[:, :], T.cst[:, :], T.b1[:, 0:1], A.add, T.x1[:, 0:1], A.subtract, w=[t_b, t_x, t_cst])
+        use("v", t_cs1, t_w64)
+        t_fix = done("v", V.tensor_reduce(T.win[:, 64:65], T.cs1[:, :], AxisListType.X, A.max))
     t_f0 = cp(T.fr[:, 0:288], T.win[:, 0:640].indirect(T.gl[:, 0:18]), w=[t_gl, t_fix])
     t_f1 = act(T.fr[:, 288:576], T.win[:, 0:640].indirect(T.gl[:, 18:36]), w=[t_gl, t_fix])
 
@@ -257,34 +256,33 @@ def rank_program(g, core, T, topo):
     use("g", t_f0, t_f1)
     g.remote_dma_fused(trs, local_sem=T.sem.ml)
 
-    t_own = t_exc
-    if q < 7:
-        t_own = act(T.ex[:, 4 * q + 4:4 * q + 8], T.exs[:, :], w=[t_exs])
     t_me = act(T.land[:, SLOTS * q:SLOTS * q + SLOTS], T.fr[:, SLOTS * q:SLOTS * q + SLOTS], w=[t_f0, t_f1])
+    ts(T.pj[:, 0:1], p0, 1, A.logical_shift_right, 7, A.bitwise_and)
+    t = ts(T.pj[:, 1:2], p0, 1, A.bitwise_and)
     ms(T.d8[:, 0:1], 576.0)
     ms(T.cum[:, 0:1], 0.0)
+    t_pf = cp(T.pf[:, 7:9], T.pj[:, 0:2], w=[t])
     t_ls = ms(T.land[:, NF:NF + 8], -2.0)
-    ts(T.elist[:, :], T.zr[:, 0:4], pf(6), A.add)
-    t_prm = ts(T.prm[:, :], T.pmi[:, :], pf(1), A.add, w=[i_pm])
-    ts(col(10), pf(7), 64.0, A.mult)
+    ts(T.elist[:, :], T.zr[:, 0:4], pf(4), A.add)
+    t_prm = ts(T.prm[:, :], T.pmi[:, :], pf(2), A.add, w=[i_pm])
+    ms(T.zr[:, 32:128], 0.0)
+    t_d8 = tt(T.d8[:, 1:8], T.ba[:, 1:8], T.ba[:, 0:7], A.subtract)
+    ts(col(10), pf(7), 64.0, A.mult, w=[t_pf])
     ts(col(11), pf(7), 8.0, A.mult)
+    t_dl8 = ts(T.dl8[:, :], T.d8[:, :], -0.125, A.mult, 72.0, A.add, w=[t_d8])
+    t_de = act(T.de[:, :], T.dl8[:, 0:8].indirect(T.elist[:, 0:4]), w=[t_dl8])
     ts(col(12), pf(8), 4.0, A.mult)
     ts(col(13), pf(8), 4.0, A.mult, -32.5, A.add)
     t = ts(col(14), pf(8), 4.0, A.mult, -31.5, A.add)
+    t_te = cp(T.te[:, :], T.xa[:, 0:8].indirect(T.elist[:, 0:4]))
     ts(T.tq[:, :], T.ti[:, :], col(10), A.add, col(13), A.add, w=[i_ti, t])
-    ts(T.tq1[:, :], T.ti[:, :], col(10), A.add, col(14), A.add)
+    t = ts(T.tq1[:, :], T.ti[:, :], col(10), A.add, col(14), A.add)
     ts(T.bs[:, 0:8], T.bsi[:, 0:8], col(11), A.add, col(12), A.add, w=[i_bs])
     ts(T.bs[:, 8:16], T.bsi[:, 8:16], col(12), A.add)
-    t_xa = scan(T.xa[:, :], T.ex[:, 0:32:4], T.zr[:, 0:8], 0.0, A.add, A.add, w=[EXA, t_own])
-    t = ts(T.ba[:, :], T.xa[:, :], MAGIC, A.add, MAGIC, A.subtract, w=[t_xa])
-    t = tt(T.d8[:, 1:8], T.ba[:, 1:8], T.ba[:, 0:7], A.subtract, w=[t])
-    t_dl8 = ts(T.dl8[:, :], T.d8[:, :], -0.125, A.mult, 72.0, A.add, w=[t])
-    t_de = act(T.de[:, :], T.dl8[:, 0:8].indirect(T.elist[:, 0:4]), w=[t_dl8])
-    t_te = cp(T.te[:, :], T.xa[:, 0:8].indirect(T.elist[:, 0:4]))
-    t_ge = tt(T.ge[:, :], T.tq[:, :], T.te[:, :], A.is_ge, w=[t_te])
+    t_ge = tt(T.ge[:, :], T.tq[:, :], T.te[:, :], A.is_ge, w=[t_te, t])
     t_eq = tt(T.eq[:, :], T.tq1[:, :], T.te[:, :], A.is_equal)
-    tt(T.pq[:, 64:128], T.eq[:, :], T.k72[:, :], A.mult, w=[t_eq, i_k72])
     t = tt(T.pq[:, 0:64], T.ge[:, :], T.de[:, :], A.mult, w=[t_ge, t_de])
+    t = tt(T.pq[:, 64:128], T.eq[:, :], T.k72[:, :], A.mult, w=[t_eq, i_k72])
     t = scan(T.cum[:, 1:129], T.pq[:, :], T.zr[:, 0:128], 0.0, A.add, A.add, w=[t])
     t = tt(T.dif[:, :], T.cum[:, 8:129:8], T.cum[:, 0:128:8], A.subtract, w=[t])
     t = tt(T.off[:, :], T.dif[:, :], T.bs[:, :], A.add, w=[t])

@@ -1,21 +1,21 @@
 from concourse.bass import DstId, RemoteDMATransfer
 from concourse.mybir import dt, AluOpType, AxisListType, ActivationFunctionType
 
-SLOTS = 72
+SLOTS = 64
 NF = 8 * SLOTS
 NEG = -4194304.0
-MAGIC = 805306368.0
-WIN = 1696
+WIN = 1800
 
 _SBUF = {
-    "int32": "pi 16 pj 16 raw 64 v 520",
-    "bfloat16": "mi 128 mb 128 m1 128 ml1 128 m5 128 m70 128 m71 128 mki 128 mk 128 r16 2 c1 32 zo 34 ho 32 szh 68",
-    "uint16": "codel 32 voffl 32 slotl 34 gl 36 prm 8 elist 4 lst 16",
-    "float32": "pf 16 cols 16 cwin 96 ctmp 64 zr 128 tf 64 of 64 rl2 32 ct 32 co 32 nz 34 nh 32 dd 32 s3 32 jc 34 nj 34 "
-               "slf 34 vf 32 oh 512 aa 512 bb 512 ohl 16 el1 16 sc 528 win %d exs 2 ex 36 kc 16 cm 16 cs1 16 "
-               "ff 72 fd 36 fe 36 cst 36 fr %d land %d ti 64 tq 64 tq1 64 k72 64 bsi 16 bs 16 "
-               "pmi 8 xa 8 ba 8 d8 8 dl8 8 te 64 de 64 ge 64 eq 64 pq 128 cum 132 dif 16 off 16 sec 128 ym 128 "
-               "zt 128 zf0 64 zf1 64" % (WIN, NF, NF + 8),
+    "int32": "pi 16 pj 16 raw 64 v 520 g1 32 g2 32",
+    "bfloat16": "mi 128 mb 128 m0 128 m1 128 mn1 128 ml1 128 m5 128 m70 128 m71 128 mki 128 mk 128 c1 32 "
+                "xT 64 x 66 sd0 66 sx 66 uT 32",
+    "uint16": "codel 32 voffl 32 slotl 34 gl 32 prm 8 elist 4 lst 16",
+    "float32": "pf 16 cols 16 cwin 96 ctmp 64 zr 128 tf 32 fT 32 fO 32 rl2 32 ct 32 co 32 nz 34 jc 34 nj 34 "
+               "slf 34 vf 32 oh 512 aa 512 bb 512 ohl 16 el1 16 sc 528 win %d exs 4 ex 36 ikc 16 kc 16 cm 16 cs1 16 "
+               "fixc 1 ff 32 cst 32 fr %d land %d ti 64 tq 64 tq1 64 k8 64 bsi 16 bs 16 "
+               "pmi 8 xa 8 xb 8 xe 8 te 64 eq 64 pq 128 cum 132 dif 16 off 16 sec 128 ym 128 "
+               "zt 128 zf0 64 zf1 64" % (WIN, NF, NF + 64),
 }
 SCRATCH = {}
 for _d, _s in _SBUF.items():
@@ -103,66 +103,67 @@ def rank_program(g, core, T, topo):
     i_mb = iota(T.mb[:, :], [[1, 8], [0, 16]], 0, 0)
     i_mi = iota(T.mi[:, :], [[1, 128]], 0, 0)
     i_mk = iota(T.mki[0:1, :], [[0, 4], [1, 32]], 0, 0)
-    i_jc = iota(T.jc[:, 0:33], [[16, 33]], 577, 0)
-    i_ff = iota(T.ff[:, :], [[8, 8], [64, 9]], 32, 0)
-    i_kc = iota(T.kc[:, :], [[-2, 16]], -2, 0)
-    i_v = iota(T.v[:, 512:520], [[-1, 8]], -1, 0, False)
 
-    ms(T.zr[:, 0:32], 0.0)
-    ms(T.szh[:, 0:68:34], 0.0)
-    ms(T.r16[0:1, 0:2], 16.0)
+    t_sd = ms(T.sd0[:, 0:65], 1.0)
+    t_win0 = ms(T.win[:, 512:640], -2.0)
     p0 = T.pi[:, 0:1]
-    ts(T.pi[:, 1:2], p0, 31, A.bitwise_and, w=[t_pi])
+    ts(T.pi[:, 5:6], p0, 4, A.logical_shift_right, w=[t_pi])
+    ts(T.pi[:, 1:2], p0, 31, A.bitwise_and)
     ts(T.pi[:, 2:3], p0, 15, A.bitwise_and)
     ts(T.pi[:, 3:4], p0, 3, A.logical_shift_right, 1, A.bitwise_and)
-    ts(T.pi[:, 4:5], p0, 7, A.bitwise_and)
-    t = ts(T.pi[:, 5:6], p0, 4, A.logical_shift_right)
+    t = ts(T.pi[:, 4:5], p0, 7, A.bitwise_and)
+    t_sd = ms(T.sd0[:, 32:33], 0.0, w=[t_sd])
+    ms(T.ex[:, 0:1], -1.0)
     t_pf = cp(T.pf[:, 0:6], T.pi[:, 0:6], w=[t])
-    ts(col(0), pf(1), 31.0, A.is_equal, w=[t_pf])
+    t_mn = ts(T.mn1[:, :], T.mb[:, :], pf(5), A.is_equal, -1.0, A.mult, w=[i_mb, t_pf])
     ts(col(1), pf(1), 31.0, A.not_equal)
-    ts(col(2), pf(5), -1.0, A.add)
-    t = ts(col(3), pf(0), 1.0, A.add)
-    t_m1 = ts(T.m1[:, :], T.mb[:, :], pf(5), A.is_equal, w=[i_mb])
-    ts(T.m70[:, :], T.mb[:, :], col(2), A.is_equal, col(0), A.mult, w=[t])
-    ts(T.m71[:, :], T.mb[:, :], pf(5), A.is_equal, col(0), A.mult)
-    ts(T.m5[:, :], T.mi[:, :], col(3), A.is_equal, col(1), A.mult, w=[i_mi])
-    t_exc = ms(T.ex[:, 0:1], -32.5)
-    t_mk = ts(T.mk[0:1, :], T.mki[0:1, :], 0.0, A.is_equal, w=[i_mk])
-    ts(T.zo[:, 32:33], pf(2), 0.0, A.is_equal)
-    ts(T.nz[:, 32:33], pf(2), 0.0, A.not_equal)
-    ms(T.sc[:, 0:1], -2.0)
-    ms(T.sc[:, 513:528], -2.0)
-    t_win0 = ms(T.win[:, 512:640], -2.0)
+    t_c3 = ts(col(3), pf(0), 1.0, A.add)
+    ts(col(0), pf(1), 31.0, A.is_equal)
+    t_c2 = ts(col(2), pf(5), -1.0, A.add)
+    t_c4 = ts(col(4), pf(2), 0.0, A.is_equal)
+    t_m1 = ts(T.m1[:, :], T.mb[:, :], pf(5), A.is_equal)
+    t_x1 = ts(T.x[:, 64:65], pf(2), 0.0, A.is_equal)
+    t_m5 = ts(T.m5[:, :], T.mi[:, :], col(3), A.is_equal, col(1), A.mult, w=[i_mi, t_c3])
+    ts(T.m70[:, :], T.mb[:, :], col(2), A.is_equal, col(0), A.mult, w=[t_c2])
+    t_m7 = ts(T.m71[:, :], T.mb[:, :], pf(5), A.is_equal, col(0), A.mult)
+    t_m0 = ts(T.m0[:, :], T.mb[:, :], pf(5), A.is_equal, col(4), A.mult, w=[t_c4])
 
-    t = act(col(7), pf(4), None, pf(3), 2.0, w=[t_pf])
-    t_c9 = act(col(9), pf(4), None, 0.5)
+    t_c7 = act(col(7), pf(4), None, pf(3), 2.0, w=[t_pf])
     act(T.cwin[:, 32:64], T.mi[:, 0:32], None, -2.0, 2097152.0, w=[i_mi])
-    t_ct = act(T.ctmp[:, 32:64], T.mi[:, 0:32], ACT.Relu, 16.0, -1.0)
-    t_c7 = act(T.ctmp[:, 0:32], T.mi[:, 0:32], ACT.Abs, col(7), -1.0, w=[t])
-    t_jc = act(T.jc[:, 0:33], T.jc[:, 0:33], None, pf(2), w=[i_jc])
-    act(T.cwin[:, 64:96], T.ctmp[:, 32:64], None, 0.0, NEG, w=[t_ct])
-    t_cw = act(T.cwin[:, 0:32], T.ctmp[:, 0:32], None, 0.0, NEG, w=[t_c7])
-    t_kc = act(T.kc[:, :], T.kc[:, :], None, col(7), w=[i_kc])
+    t_cb = act(T.ctmp[:, 0:32], T.mi[:, 0:32], ACT.Abs, col(7), -1.0, w=[t_c7])
+    t_mk = act(T.mk[0:1, :], T.mki[0:1, :], ACT.Relu, 16.0, -16.0, w=[i_mk])
+    t_cw = act(T.cwin[:, 0:32], T.ctmp[:, 0:32], None, 0.0, NEG, w=[t_cb])
+    for a in (384, 256, 128):
+        act(T.win[:, a:a + 128], T.win[:, 512:640], w=[t_win0])
 
-    use("g", t_m1)
-    t_l = done("g", g.affine_select(T.ml1[:, :], T.m1[:, :], [[1, 128]], A.is_ge, 0.0, 0, -1))
+    use("g", t_mn)
+    t_l = done("g", g.affine_select(T.ml1[:, :], T.mn1[:, :], [[-1, 128]], A.is_gt, 0.0, 0, 1))
+    i_jc = iota(T.jc[:, 0:33], [[16, 33]], 577, 1)
+    i_v = iota(T.v[:, 512:520], [[-1, 8]], 1, 0, False)
 
-    t_tf = cp(T.tf[:, 0:32], T.raw[:, 0:32], w=[LDR])
+    t_tf = cp(T.tf[:, :], T.raw[:, 0:32], w=[LDR])
     t_rl2 = ts(T.rl2[:, :], T.raw[:, 0:32], 2.0, A.is_equal)
-    t_of = tr(T.of[:, 0:32], T.tf[:, 0:32], w=[t_tf])
-    t_s1 = scan(T.c1[:, :], T.rl2[:, :], T.tf[:, 0:32], 0.0, A.mult, A.add, w=[t_rl2])
-    t_zo = ts(T.zo[:, 0:32], T.of[:, 0:32], 0.0, A.is_equal, w=[t_of])
-    t_nz = ts(T.nz[:, 0:32], T.of[:, 0:32], 1.0, A.min)
-    t_sz = scan(T.szh[:, 1:33], T.zo[:, 0:32], T.zr[:, 0:32], 0.0, A.add, A.add, w=[t_zo])
-    mm(T.pa[:, 0:2], T.mk[0:1, :], T.r16[0:1, 0:2], True, False, w=[t_mk])
-    t_pa = mm(T.pa[:, 0:2], T.m5[:, :], T.c1[:, 15:32:16], False, True, w=[t_s1])
-    mm(T.pb[:, 1:2], T.m70[:, :], T.c1[:, 15:16], True, False)
+    ts(T.xT[:, 32:64], T.raw[:, 0:32], 0.0, A.is_equal)
+    t_xT = ts(T.xT[:, 0:32], T.raw[:, 32:64], 2.0, A.is_equal, w=[LDD])
+    t_c1 = scan(T.c1[:, :], T.rl2[:, :], T.tf[:, :], 0.0, A.mult, A.add, w=[t_rl2])
+    t_uT = ts(T.uT[:, :], T.raw[:, 32:64], 2.0, A.is_lt, 516.0, A.mult)
+    t_x = tr(T.x[:, 0:64], T.xT[:, :], w=[t_xT])
+    mm(T.pa[:, 0:2], T.mk[0:1, :], T.m1[0:1, 0:2], True, False, w=[t_mk, t_m1])
+    t_pa = mm(T.pa[:, 0:2], T.m5[:, :], T.c1[:, 15:32:16], False, True, w=[t_c1, t_m5])
+    t_fT = tt(T.fT[:, :], T.uT[:, :], T.raw[:, 32:64], A.subtract, w=[t_uT])
+    t_sx = scan(T.sx[:, 0:65], T.sd0[:, 0:65], T.x[:, 0:65], 0.0, A.mult, A.add, w=[t_x, t_sd, t_x1])
+    scan(T.ct[:, 0:16], T.rl2[:, 0:16], T.tf[:, 0:16], T.pa[:, 0:1], A.mult, A.add, w=[t_pa])
+    t_ct = scan(T.ct[:, 16:32], T.rl2[:, 16:32], T.tf[:, 16:32], T.pa[:, 1:2], A.mult, A.add)
+    t_fO = tr(T.fO[:, :], T.fT[:, :], w=[t_fT])
+    mm(T.pb[:, 1:2], T.m70[:, :], T.c1[:, 15:16], True, False, w=[t_m7])
     mm(T.pb[:, 1:2], T.m71[:, :], T.c1[:, 31:32], False, True)
-    t_pb = mm(T.pb[:, 0:1], T.m1[:, :], T.szh[:, 32:33], True, True, w=[t_sz])
-    mm(T.pc[:, 0:33], T.m1[:, :], T.szh[:, 0:33], True, False)
-    t_pc = mm(T.pc[:, 0:33], T.ml1[:, :], T.zo[:, 0:33], False, True, w=[t_zo, t_l])
+    mm(T.pb[:, 2:3], T.m0[:, :], T.x[:, 32:33], True, True, w=[t_x, t_m0])
+    t_pb = mm(T.pb[:, 0:1], T.m1[:, :], T.sx[:, 63:64], True, True, w=[t_sx])
+    mm(T.pd[:, 0:32], T.ml1[:, :], T.x[:, 0:32], True, False, w=[t_l])
+    t_pd = mm(T.pd[:, 0:32], T.m1[:, :], T.sx[:, 0:32], False, True)
+    mm(T.pc[:, 0:33], T.ml1[:, :], T.x[:, 32:65], True, False, w=[t_x1])
+    t_pc = mm(T.pc[:, 0:33], T.m1[:, :], T.sx[:, 32:65], False, True)
 
-    t_exs = act(T.exs[:, :], T.pb[:, 0:2], w=[t_pb])
     others = [c for c in T.cores if c != core]
 
     def dst_id(c):
@@ -175,69 +176,72 @@ def rank_program(g, core, T, topo):
             m &= topo.mask(src, c)
         return m
 
-    if q < 7:
-        use("g", t_exs)
-        o = 4 * (q + 1)
-        g.remote_dma_fused([RemoteDMATransfer(dst_ids=[dst_id(c) for c in others],
-                                              dma_engine_mask=common(core, others), remote_sem=T.sem.exa,
-                                              src=T.exs[:, :], dsts=[T.ex[:, o:o + 2] for _ in others])],
-                           local_sem=T.sem.exl)
-    EXA = ("exa", sum(bin(common(c, [d for d in T.cores if d != c])).count("1") for c in T.cores[0:7] if c != core))
+    t_co = tr(T.co[:, :], T.ct[:, :], w=[t_ct])
+    t_exs = cp(T.exs[:, 0:3], T.pb[:, 0:3], w=[t_pb])
+    use("g", t_exs)
+    o = 4 * (q + 1)
+    g.remote_dma_fused([RemoteDMATransfer(dst_ids=[dst_id(c) for c in others],
+                                          dma_engine_mask=common(core, others), remote_sem=T.sem.exa,
+                                          src=T.exs[:, 0:2], dsts=[T.ex[:, o:o + 2] for _ in others])],
+                       local_sem=T.sem.exl)
+    EXA = ("exa", sum(bin(common(c, [d for d in T.cores if d != c])).count("1") for c in others))
+    i_ff = iota(T.ff[:, :], [[8, 8], [128, 4]], 0, 0)
+    i_kc = iota(T.ikc[:, :], [[-2, 16]], -2, 0)
     i_ti = iota(T.ti[:, :], [[1, 4], [512, 2], [0, 8]], 8 * q, 0)
-    i_k72 = iota(T.k72[:, :], [[0, 8], [72, 8]], -576, 0)
-    iota(T.bsi[:, 0:8], [[1, 4], [64, 2]], 8, 0)
-    i_bs = iota(T.bsi[:, 8:16], [[1, 4], [0, 2]], 576, 0)
+    i_k8 = iota(T.k8[:, :], [[0, 8], [1, 8]], -8, 0)
+    i_bs = iota(T.bsi[:, :], [[512, 2], [1, 4], [0, 2]], 0, 0)
     i_pm = iota(T.pmi[:, :], [[16, 2], [32, 4]], 0, 0)
 
-    scan(T.ct[:, 0:16], T.rl2[:, 0:16], T.tf[:, 0:16], T.pa[:, 0:1], A.mult, A.add, w=[t_pa])
-    t = scan(T.ct[:, 16:32], T.rl2[:, 16:32], T.tf[:, 16:32], T.pa[:, 1:2], A.mult, A.add)
-    t_nj = tt(T.nj[:, 0:33], T.nz[:, 0:33], T.jc[:, 0:33], A.mult, w=[t_nz, t_jc])
-    t = tr(T.co[:, :], T.ct[:, :], w=[t])
-    t_fd = tt(T.fd[:, :], T.ff[:, 1:72:2], T.ff[:, 0:72:2], A.subtract, w=[i_ff])
-    t_code = cp(T.codel[:, :], T.co[:, :], w=[t])
-    t_oh = act(T.oh[:, :], T.cwin[:, 0:32].indirect(T.codel[:, 0:32]), w=[t_code, t_cw])
-    t_ohl = act(T.ohl[:, :], T.cwin[:, 64:96].indirect(T.codel[:, 0:1]))
-    t_aa = act(T.aa[:, :], T.cwin[:, 32:64].indirect(T.codel[:, 0:32]))
-    t_win = act(T.win[:, 0:512], T.oh[:, :], None, -2.0, 0.0, w=[t_oh])
-    t_own = t_exc
-    if q < 7:
-        t_own = act(T.ex[:, 4 * q + 4:4 * q + 6], T.exs[:, :], w=[t_exs])
-    t_tfd = cp(T.tf[:, 32:64], T.raw[:, 32:64], w=[LDD])
-    t_slf = tt(T.slf[:, 0:33], T.pc[:, 0:33], T.nj[:, 0:33], A.add, w=[t_pc, t_nj])
-    t_ofd = tr(T.of[:, 32:64], T.tf[:, 32:64], w=[t_tfd])
-    t_slot = ts(T.slotl[:, 0:33], T.slf[:, 0:33], 63.0, A.add, w=[t_slf])
-    t_ho = ts(T.ho[:, :], T.of[:, 32:64], 2.0, A.is_equal, w=[t_ofd])
-    ts(T.nh[:, :], T.of[:, 32:64], -1.0, A.mult, 2.0, A.add)
-    t_sh = scan(T.szh[:, 35:67], T.ho[:, :], T.zr[:, 0:32], 0.0, A.add, A.add, w=[t_ho])
-    mm(T.pd[:, 0:32], T.ml1[:, :], T.ho[:, :], True, False, w=[t_ho])
-    t_pd = mm(T.pd[:, 0:32], T.m1[:, :], T.szh[:, 34:66], False, True, w=[t_sh])
-    t_dd = ts(T.dd[:, :], T.of[:, 32:64], 2.0, A.is_lt, 512.0, A.mult)
-    ts(T.fe[:, :], T.fd[:, :], pf(3), A.mult, col(9), A.add, w=[t_fd, t_c9])
-    t_s3 = tt(T.s3[:, :], T.dd[:, :], T.nh[:, :], A.add, w=[t_dd])
-    t = tt(T.vf[:, :], T.pd[:, 0:32], T.s3[:, :], A.max, w=[t_pd, t_s3])
-    t_cst = tt(T.cst[:, :], T.fe[:, :], T.ff[:, 0:72:2], A.add)
+    t_code = cp(T.codel[:, :], T.co[:, :], w=[t_co])
+    t_oh0 = act(T.oh[:, 0:256], T.cwin[:, 0:32].indirect(T.codel[:, 0:16]), w=[t_code, t_cw])
+    t_oh1 = act(T.oh[:, 256:512], T.cwin[:, 0:32].indirect(T.codel[:, 16:32]))
+    t_aa0 = act(T.aa[:, 0:256], T.cwin[:, 32:64].indirect(T.codel[:, 0:16]))
+    t_aa1 = act(T.aa[:, 256:512], T.cwin[:, 32:64].indirect(T.codel[:, 16:32]))
+    t_win = act(T.win[:, 64:128], T.win[:, 512:576])
+    t = tt(T.vf[:, :], T.pd[:, 0:32], T.fO[:, :], A.max, w=[t_pd, t_fO])
+    t_nz = ts(T.nz[:, 0:33], T.x[:, 32:65], 0.0, A.is_equal)
     t_voff = ts(T.voffl[:, :], T.vf[:, :], -1.0, A.add, w=[t])
+    t_nj = tt(T.nj[:, 0:33], T.nz[:, 0:33], T.jc[:, 0:33], A.mult, w=[t_nz, i_jc])
+    ms(T.sc[:, 0:1], -2.0)
+    t_sc0 = ms(T.sc[:, 513:528], -2.0)
 
-    t_bb = tt(T.bb[:, :], T.v[:, 0:520].indirect(T.voffl[:, 0:32]), T.oh[:, :], A.add, w=[LDV, i_v, t_voff, t_oh])
-    t = scan(T.sc[:, 1:513], T.aa[:, :], T.bb[:, :], -2.0, A.min, A.max, w=[t_bb, t_aa])
-    t_el = tt(T.el1[:, :], T.v[:, 0:520].indirect(T.voffl[:, 0:1]), T.ohl[:, :], A.add, w=[t_ohl])
-    t_scat = cp(T.win[:, 0:WIN].indirect(T.slotl[:, 0:33]), T.sc[:, :], w=[t, t_slot, t_win0, t_win])
+    t_b0 = tt(T.bb[:, 0:256], T.v[:, 0:520].indirect(T.voffl[:, 0:16]), T.oh[:, 0:256], A.add,
+              w=[LDV, i_v, t_voff, t_oh0])
+    t_slf = tt(T.slf[:, 0:33], T.pc[:, 0:33], T.nj[:, 0:33], A.add, w=[t_pc, t_nj])
+    t_b1 = tt(T.bb[:, 256:512], T.v[:, 0:520].indirect(T.voffl[:, 16:32]), T.oh[:, 256:512], A.add, w=[t_oh1])
+    t_slot = ts(T.slotl[:, 0:33], T.slf[:, 0:33], 63.0, A.add, w=[t_slf])
+    t = scan(T.sc[:, 1:257], T.aa[:, 0:256], T.bb[:, 0:256], -2.0, A.min, A.max, w=[t_b0, t_aa0])
+    t_zr = ms(T.zr[:, 0:8], 0.0)
+    t = scan(T.sc[:, 257:513], T.aa[:, 256:512], T.bb[:, 256:512], T.sc[:, 256:257], A.min, A.max,
+             w=[t_b1, t_aa1, t])
+    t_scat = cp(T.win[:, 0:WIN].indirect(T.slotl[:, 0:33]), T.sc[:, :], w=[t, t_slot, t_sc0, t_win0, t_win])
+
+    t_c9 = act(col(9), pf(3), None, pf(4), 64.0)
+    t_ca = act(T.ctmp[:, 32:64], T.mi[:, 0:32], ACT.Relu, 16.0, -1.0)
+    t_own = act(T.ex[:, o:o + 2], T.exs[:, 0:2], w=[t_exs])
+    t_cw = act(T.cwin[:, 64:96], T.ctmp[:, 32:64], None, 0.0, NEG, w=[t_ca])
+    t_cst = act(T.cst[:, :], T.ff[:, :], None, col(9), w=[i_ff, t_c9])
+    t_ohl = act(T.ohl[:, :], T.cwin[:, 64:96].indirect(T.codel[:, 0:1]), w=[t_cw])
+    t_kc = act(T.kc[:, :], T.ikc[:, :], None, col(7), w=[i_kc])
 
     if q:
-        t_w64 = act(T.cs1[:, 15:16], T.win[:, 64:65], w=[t_scat])
-    t_xa = scan(T.xa[:, :], T.ex[:, 0:32:4], T.zr[:, 0:8], 0.0, A.add, A.add, w=[EXA, t_own])
+        t_el = tt(T.el1[:, :], T.v[:, 0:520].indirect(T.voffl[:, 0:1]), T.ohl[:, :], A.add, w=[t_ohl])
+    t_xa = scan(T.xa[:, :], T.ex[:, 0:32:4], T.zr[:, 0:8], 0.0, A.add, A.add, w=[EXA, t_own, t_zr])
     if q:
         t_cm = ts(T.cm[:, :], T.kc[:, :], T.ex[:, 4 * q + 1:4 * q + 2], A.not_equal, NEG, A.mult, w=[t_kc])
-    t_ba = ts(T.ba[:, :], T.xa[:, :], MAGIC, A.add, MAGIC, A.subtract, w=[t_xa])
+    t_g1 = ts(T.g1[:, :], T.cst[:, :], T.xa[:, q:q + 1], A.subtract, T.exs[:, 2:3], A.subtract, w=[t_xa, t_cst])
     if q:
         t_cs1 = tt(T.cs1[:, 0:15], T.cm[:, 0:15], T.el1[:, 0:15], A.add, w=[t_cm, t_el])
-    t_gl = ts(T.gl[:, :], T.cst[:, :], T.ba[:, q:q + 1], A.add, T.xa[:, q:q + 1], A.subtract, w=[t_ba, t_cst])
+    t_g2 = ts(T.g2[:, :], T.g1[:, :], NF - 1, A.bitwise_and, w=[t_g1])
     t_fix = t_scat
     if q:
-        use("v", t_cs1, t_w64)
-        t_fix = done("v", V.tensor_reduce(T.win[:, 64:65], T.cs1[:, :], AxisListType.X, A.max))
-    t_f0 = cp(T.fr[:, 0:288], T.win[:, 0:640].indirect(T.gl[:, 0:18]), w=[t_gl, t_fix])
-    t_f1 = act(T.fr[:, 288:576], T.win[:, 0:640].indirect(T.gl[:, 18:36]), w=[t_gl, t_fix])
+        use("v", t_cs1)
+        t = done("v", V.tensor_reduce(T.fixc[:, :], T.cs1[:, 0:15], AxisListType.X, A.max))
+    t_gl = ts(T.gl[:, :], T.g2[:, :], T.exs[:, 2:3], A.add, w=[t_g2])
+    if q:
+        t_fix = tt(T.win[:, 64:65], T.win[:, 64:65], T.fixc[:, :], A.max, w=[t, t_scat])
+    t_f0 = cp(T.fr[:, 0:256], T.win[:, 64:640].indirect(T.gl[:, 0:16]), w=[t_gl, t_fix])
+    t_f1 = act(T.fr[:, 256:512], T.win[:, 64:640].indirect(T.gl[:, 16:32]), w=[t_gl, t_fix])
 
     near = [d for d in range(8) if d != q and topo.die(T.cores[d]) == topo.die(core)]
     far = [d for d in range(8) if d != q and topo.die(T.cores[d]) != topo.die(core)]
@@ -259,42 +263,38 @@ def rank_program(g, core, T, topo):
     t_me = act(T.land[:, SLOTS * q:SLOTS * q + SLOTS], T.fr[:, SLOTS * q:SLOTS * q + SLOTS], w=[t_f0, t_f1])
     ts(T.pj[:, 0:1], p0, 1, A.logical_shift_right, 7, A.bitwise_and)
     t = ts(T.pj[:, 1:2], p0, 1, A.bitwise_and)
-    ms(T.d8[:, 0:1], 576.0)
+    t_xb = ts(T.xb[:, 1:8], T.ex[:, 8:36:4], 512.0, A.is_ge, 0.25, A.mult)
+    ts(T.xe[:, 0:1], T.xa[:, 7:8], T.ex[:, 32:33], A.add, 0.25, A.add)
+    t_el = ts(T.elist[:, :], T.zr[:, 0:4], pf(4), A.add)
+    t_pj = cp(T.pf[:, 8:10], T.pj[:, 0:2], w=[t])
+    t_xe = tt(T.xe[:, 1:8], T.xa[:, 1:8], T.xb[:, 1:8], A.add, w=[t_xb])
+    t_ls = ms(T.land[:, NF:NF + 64], -2.0)
+    ts(col(12), pf(9), 4.0, A.mult, w=[t_pj])
+    t = ts(col(13), pf(9), 0.0625, A.mult)
+    t_te = cp(T.te[:, :], T.xe[:, 0:8].indirect(T.elist[:, 0:4]), w=[t_xe, t_el])
+    ts(col(10), pf(8), 64.0, A.mult, col(12), A.add, w=[t])
+    t = ts(col(11), pf(8), 0.125, A.mult, col(13), A.add)
+    t_bs = act(T.bs[:, :], T.bsi[:, :], None, col(11), 0.015625, w=[t, i_bs])
     ms(T.cum[:, 0:1], 0.0)
-    t_pf = cp(T.pf[:, 7:9], T.pj[:, 0:2], w=[t])
-    t_ls = ms(T.land[:, NF:NF + 8], -2.0)
-    ts(T.elist[:, :], T.zr[:, 0:4], pf(4), A.add)
+    t_q1 = ts(T.tq1[:, :], T.ti[:, :], col(10), A.add, w=[t, i_ti])
+    t_q0 = ts(T.tq[:, :], T.ti[:, :], col(10), A.add, -0.5, A.add)
+    t_zr = ms(T.zr[:, 8:128], 0.0)
+    t_eq = tt(T.eq[:, :], T.tq1[:, :], T.te[:, :], A.is_equal, w=[t_te, t_q1])
+    t2 = tt(T.pq[:, 0:64], T.tq[:, :], T.te[:, :], A.is_ge, w=[t_q0])
+    t = tt(T.pq[:, 64:128], T.eq[:, :], T.k8[:, :], A.mult, w=[t_eq, i_k8])
     t_prm = ts(T.prm[:, :], T.pmi[:, :], pf(2), A.add, w=[i_pm])
-    ms(T.zr[:, 32:128], 0.0)
-    t_d8 = tt(T.d8[:, 1:8], T.ba[:, 1:8], T.ba[:, 0:7], A.subtract)
-    ts(col(10), pf(7), 64.0, A.mult, w=[t_pf])
-    ts(col(11), pf(7), 8.0, A.mult)
-    t_dl8 = ts(T.dl8[:, :], T.d8[:, :], -0.125, A.mult, 72.0, A.add, w=[t_d8])
-    t_de = act(T.de[:, :], T.dl8[:, 0:8].indirect(T.elist[:, 0:4]), w=[t_dl8])
-    ts(col(12), pf(8), 4.0, A.mult)
-    ts(col(13), pf(8), 4.0, A.mult, -32.5, A.add)
-    t = ts(col(14), pf(8), 4.0, A.mult, -31.5, A.add)
-    t_te = cp(T.te[:, :], T.xa[:, 0:8].indirect(T.elist[:, 0:4]))
-    ts(T.tq[:, :], T.ti[:, :], col(10), A.add, col(13), A.add, w=[i_ti, t])
-    t = ts(T.tq1[:, :], T.ti[:, :], col(10), A.add, col(14), A.add)
-    ts(T.bs[:, 0:8], T.bsi[:, 0:8], col(11), A.add, col(12), A.add, w=[i_bs])
-    ts(T.bs[:, 8:16], T.bsi[:, 8:16], col(12), A.add)
-    t_ge = tt(T.ge[:, :], T.tq[:, :], T.te[:, :], A.is_ge, w=[t_te, t])
-    t_eq = tt(T.eq[:, :], T.tq1[:, :], T.te[:, :], A.is_equal)
-    t = tt(T.pq[:, 0:64], T.ge[:, :], T.de[:, :], A.mult, w=[t_ge, t_de])
-    t = tt(T.pq[:, 64:128], T.eq[:, :], T.k72[:, :], A.mult, w=[t_eq, i_k72])
-    t = scan(T.cum[:, 1:129], T.pq[:, :], T.zr[:, 0:128], 0.0, A.add, A.add, w=[t])
+    t = scan(T.cum[:, 1:129], T.pq[:, :], T.zr[:, 0:128], 0.0, A.add, A.add, w=[t, t2, t_zr])
     t = tt(T.dif[:, :], T.cum[:, 8:129:8], T.cum[:, 0:128:8], A.subtract, w=[t])
-    t = tt(T.off[:, :], T.dif[:, :], T.bs[:, :], A.add, w=[t])
-    t_lst = ts(T.lst[:, :], T.off[:, :], float(NF + 7), A.min, w=[t])
+    t = tt(T.off[:, :], T.dif[:, :], T.bs[:, :], A.add, w=[t, t_bs])
+    t_lst = ts(T.lst[:, :], T.off[:, :], float(SLOTS), A.mult, w=[t])
 
     MA = ("ma", 14)
-    t_sec = act(T.sec[:, :], T.land[:, 0:NF + 8].indirect(T.lst[:, 8:16]), w=[t_lst, t_ls, t_me, MA])
-    t = tt(T.ym[:, :], T.land[:, 0:NF + 8].indirect(T.lst[:, 0:8]), T.sec[:, :], A.max,
+    t_sec = act(T.sec[:, :], T.land[:, 0:NF + 64].indirect(T.lst[:, 8:16]), w=[t_lst, t_ls, t_me, MA])
+    t = tt(T.ym[:, :], T.land[:, 0:NF + 64].indirect(T.lst[:, 0:8]), T.sec[:, :], A.max,
            w=[MA, t_lst, t_ls, t_me, t_sec])
     t_zt = tr(T.zt[:, :], T.ym[:, :], w=[t])
     t_z0 = cp(T.zf0[:, :], T.zt[:, :].indirect(T.prm[:, 0:4]), w=[t_zt, t_prm])
-    t_z1 = act(T.zf1[:, :], T.zt[:, :].indirect(T.prm[:, 4:8]), w=[t_zt])
+    t_z1 = act(T.zf1[:, :], T.zt[:, :].indirect(T.prm[:, 4:8]), w=[t_zt, t_prm])
     use("y", t_z0)
     g.sync.dma_start(T.y[0::2, :], T.zf0[:, :]).then_inc(T.sem.st, 16)
     use("s", t_z1)
@@ -303,6 +303,4 @@ def rank_program(g, core, T, topo):
     use("y", ("st", 32))
     for k in ("v", "s", "p", "g"):
         use("g", ("c" + k, cnt[k]))
-    if q < 7:
-        use("g", ("exl", bin(common(core, others)).count("1")))
-    use("g", ("ml", 14), EXA)
+    use("g", ("exl", bin(common(core, others)).count("1")), ("ml", 14), EXA)

@@ -113,20 +113,18 @@ def rank_program(g, core, T, topo):
     ts(T.pi[:, 3:4], p0, 3, A.logical_shift_right, 1, A.bitwise_and)
     t = ts(T.pi[:, 4:5], p0, 7, A.bitwise_and)
     t_sd = ms(T.sd0[:, 32:33], 0.0, w=[t_sd])
-    ms(T.ex[:, 0:1], -1.0)
     t_pf = cp(T.pf[:, 0:6], T.pi[:, 0:6], w=[t])
     t_mn = ts(T.mn1[:, :], T.mb[:, :], pf(5), A.is_equal, -1.0, A.mult, w=[i_mb, t_pf])
     ts(col(1), pf(1), 31.0, A.not_equal)
     t_c3 = ts(col(3), pf(0), 1.0, A.add)
     ts(col(0), pf(1), 31.0, A.is_equal)
     t_c2 = ts(col(2), pf(5), -1.0, A.add)
-    t_c4 = ts(col(4), pf(2), 0.0, A.is_equal)
-    t_m1 = ts(T.m1[:, :], T.mb[:, :], pf(5), A.is_equal)
     t_x1 = ts(T.x[:, 64:65], pf(2), 0.0, A.is_equal)
+    t_m1 = ts(T.m1[:, :], T.mb[:, :], pf(5), A.is_equal)
     t_m5 = ts(T.m5[:, :], T.mi[:, :], col(3), A.is_equal, col(1), A.mult, w=[i_mi, t_c3])
     ts(T.m70[:, :], T.mb[:, :], col(2), A.is_equal, col(0), A.mult, w=[t_c2])
     t_m7 = ts(T.m71[:, :], T.mb[:, :], pf(5), A.is_equal, col(0), A.mult)
-    t_m0 = ts(T.m0[:, :], T.mb[:, :], pf(5), A.is_equal, col(4), A.mult, w=[t_c4])
+    t_m0 = ts(T.m0[:, :], T.m1[:, :], T.x[:, 64:65], A.mult, w=[t_m1])
 
     t_c7 = act(col(7), pf(4), None, pf(3), 2.0, w=[t_pf])
     act(T.cwin[:, 32:64], T.mi[:, 0:32], None, -2.0, 2097152.0, w=[i_mi])
@@ -146,15 +144,13 @@ def rank_program(g, core, T, topo):
     ts(T.xT[:, 32:64], T.raw[:, 0:32], 0.0, A.is_equal)
     t_xT = ts(T.xT[:, 0:32], T.raw[:, 32:64], 2.0, A.is_equal, w=[LDD])
     t_c1 = scan(T.c1[:, :], T.rl2[:, :], T.tf[:, :], 0.0, A.mult, A.add, w=[t_rl2])
-    t_uT = ts(T.uT[:, :], T.raw[:, 32:64], 2.0, A.is_lt, 516.0, A.mult)
     t_x = tr(T.x[:, 0:64], T.xT[:, :], w=[t_xT])
+    t_uT = ts(T.uT[:, :], T.raw[:, 32:64], 2.0, A.is_lt, 516.0, A.mult)
     mm(T.pa[:, 0:2], T.mk[0:1, :], T.m1[0:1, 0:2], True, False, w=[t_mk, t_m1])
     t_pa = mm(T.pa[:, 0:2], T.m5[:, :], T.c1[:, 15:32:16], False, True, w=[t_c1, t_m5])
-    t_fT = tt(T.fT[:, :], T.uT[:, :], T.raw[:, 32:64], A.subtract, w=[t_uT])
     t_sx = scan(T.sx[:, 0:65], T.sd0[:, 0:65], T.x[:, 0:65], 0.0, A.mult, A.add, w=[t_x, t_sd, t_x1])
     scan(T.ct[:, 0:16], T.rl2[:, 0:16], T.tf[:, 0:16], T.pa[:, 0:1], A.mult, A.add, w=[t_pa])
     t_ct = scan(T.ct[:, 16:32], T.rl2[:, 16:32], T.tf[:, 16:32], T.pa[:, 1:2], A.mult, A.add)
-    t_fO = tr(T.fO[:, :], T.fT[:, :], w=[t_fT])
     mm(T.pb[:, 1:2], T.m70[:, :], T.c1[:, 15:16], True, False, w=[t_m7])
     mm(T.pb[:, 1:2], T.m71[:, :], T.c1[:, 31:32], False, True)
     mm(T.pb[:, 2:3], T.m0[:, :], T.x[:, 32:33], True, True, w=[t_x, t_m0])
@@ -176,8 +172,10 @@ def rank_program(g, core, T, topo):
             m &= topo.mask(src, c)
         return m
 
-    t_co = tr(T.co[:, :], T.ct[:, :], w=[t_ct])
+    t_fT = tt(T.fT[:, :], T.uT[:, :], T.raw[:, 32:64], A.subtract, w=[t_uT])
     t_exs = cp(T.exs[:, 0:3], T.pb[:, 0:3], w=[t_pb])
+    t_co = tr(T.co[:, :], T.ct[:, :], w=[t_ct])
+    t_fO = tr(T.fO[:, :], T.fT[:, :], w=[t_fT])
     use("g", t_exs)
     o = 4 * (q + 1)
     g.remote_dma_fused([RemoteDMATransfer(dst_ids=[dst_id(c) for c in others],
@@ -185,6 +183,7 @@ def rank_program(g, core, T, topo):
                                           src=T.exs[:, 0:2], dsts=[T.ex[:, o:o + 2] for _ in others])],
                        local_sem=T.sem.exl)
     EXA = ("exa", sum(bin(common(c, [d for d in T.cores if d != c])).count("1") for c in others))
+    i_zr = iota(T.zr[:, :], [[0, 128]], 0, 0)
     i_ff = iota(T.ff[:, :], [[8, 8], [128, 4]], 0, 0)
     i_kc = iota(T.ikc[:, :], [[-2, 16]], -2, 0)
     i_ti = iota(T.ti[:, :], [[1, 4], [512, 2], [0, 8]], 8 * q, 0)
@@ -202,8 +201,10 @@ def rank_program(g, core, T, topo):
     t_nz = ts(T.nz[:, 0:33], T.x[:, 32:65], 0.0, A.is_equal)
     t_voff = ts(T.voffl[:, :], T.vf[:, :], -1.0, A.add, w=[t])
     t_nj = tt(T.nj[:, 0:33], T.nz[:, 0:33], T.jc[:, 0:33], A.mult, w=[t_nz, i_jc])
+    ts(T.pj[:, 0:1], p0, 1, A.logical_shift_right, 7, A.bitwise_and)
+    t = ts(T.pj[:, 1:2], p0, 1, A.bitwise_and)
     ms(T.sc[:, 0:1], -2.0)
-    t_sc0 = ms(T.sc[:, 513:528], -2.0)
+    t_pj = cp(T.pf[:, 8:10], T.pj[:, 0:2], w=[t])
 
     t_b0 = tt(T.bb[:, 0:256], T.v[:, 0:520].indirect(T.voffl[:, 0:16]), T.oh[:, 0:256], A.add,
               w=[LDV, i_v, t_voff, t_oh0])
@@ -211,7 +212,7 @@ def rank_program(g, core, T, topo):
     t_b1 = tt(T.bb[:, 256:512], T.v[:, 0:520].indirect(T.voffl[:, 16:32]), T.oh[:, 256:512], A.add, w=[t_oh1])
     t_slot = ts(T.slotl[:, 0:33], T.slf[:, 0:33], 63.0, A.add, w=[t_slf])
     t = scan(T.sc[:, 1:257], T.aa[:, 0:256], T.bb[:, 0:256], -2.0, A.min, A.max, w=[t_b0, t_aa0])
-    t_zr = ms(T.zr[:, 0:8], 0.0)
+    t_sc0 = ms(T.sc[:, 513:528], -2.0)
     t = scan(T.sc[:, 257:513], T.aa[:, 256:512], T.bb[:, 256:512], T.sc[:, 256:257], A.min, A.max,
              w=[t_b1, t_aa1, t])
     t_scat = cp(T.win[:, 0:WIN].indirect(T.slotl[:, 0:33]), T.sc[:, :], w=[t, t_slot, t_sc0, t_win0, t_win])
@@ -223,15 +224,21 @@ def rank_program(g, core, T, topo):
     t_cst = act(T.cst[:, :], T.ff[:, :], None, col(9), w=[i_ff, t_c9])
     t_ohl = act(T.ohl[:, :], T.cwin[:, 64:96].indirect(T.codel[:, 0:1]), w=[t_cw])
     t_kc = act(T.kc[:, :], T.ikc[:, :], None, col(7), w=[i_kc])
+    act(col(12), pf(9), None, 0.0, 4.0, w=[t_pj])
+    t = act(col(13), pf(9), None, 0.0, 0.0625)
+    act(col(10), pf(8), None, col(12), 64.0, w=[t])
+    t_c11 = act(col(11), pf(8), None, col(13), 0.125)
 
     if q:
         t_el = tt(T.el1[:, :], T.v[:, 0:520].indirect(T.voffl[:, 0:1]), T.ohl[:, :], A.add, w=[t_ohl])
-    t_xa = scan(T.xa[:, :], T.ex[:, 0:32:4], T.zr[:, 0:8], 0.0, A.add, A.add, w=[EXA, t_own, t_zr])
+    t_xa = scan(T.xa[:, 1:8], T.ex[:, 4:32:4], T.zr[:, 0:7], -1.0, A.add, A.add, w=[EXA, t_own, i_zr])
     if q:
         t_cm = ts(T.cm[:, :], T.kc[:, :], T.ex[:, 4 * q + 1:4 * q + 2], A.not_equal, NEG, A.mult, w=[t_kc])
-    t_g1 = ts(T.g1[:, :], T.cst[:, :], T.xa[:, q:q + 1], A.subtract, T.exs[:, 2:3], A.subtract, w=[t_xa, t_cst])
-    if q:
+        t_g1 = ts(T.g1[:, :], T.cst[:, :], T.xa[:, q:q + 1], A.subtract, T.exs[:, 2:3], A.subtract,
+                  w=[t_xa, t_cst])
         t_cs1 = tt(T.cs1[:, 0:15], T.cm[:, 0:15], T.el1[:, 0:15], A.add, w=[t_cm, t_el])
+    else:
+        t_g1 = ts(T.g1[:, :], T.cst[:, :], 1.0, A.add, T.exs[:, 2:3], A.subtract, w=[t_cst])
     t_g2 = ts(T.g2[:, :], T.g1[:, :], NF - 1, A.bitwise_and, w=[t_g1])
     t_fix = t_scat
     if q:
@@ -260,39 +267,34 @@ def rank_program(g, core, T, topo):
     use("g", t_f0, t_f1)
     g.remote_dma_fused(trs, local_sem=T.sem.ml)
 
+    t_q1 = act(T.tq1[:, :], T.ti[:, :], None, col(10), w=[t_c11, i_ti])
+    t_q0 = act(T.tq[:, :], T.tq1[:, :], None, -0.5, w=[t_q1])
+    t_bs = act(T.bs[:, :], T.bsi[:, :], None, col(11), 0.015625, w=[i_bs])
     t_me = act(T.land[:, SLOTS * q:SLOTS * q + SLOTS], T.fr[:, SLOTS * q:SLOTS * q + SLOTS], w=[t_f0, t_f1])
-    ts(T.pj[:, 0:1], p0, 1, A.logical_shift_right, 7, A.bitwise_and)
-    t = ts(T.pj[:, 1:2], p0, 1, A.bitwise_and)
     t_xb = ts(T.xb[:, 1:8], T.ex[:, 8:36:4], 512.0, A.is_ge, 0.25, A.mult)
-    ts(T.xe[:, 0:1], T.xa[:, 7:8], T.ex[:, 32:33], A.add, 0.25, A.add)
+    ts(T.xe[:, 0:1], T.xa[:, 7:8], T.ex[:, 32:33], A.add, 0.25, A.add, w=[t_xa, EXA])
     t_el = ts(T.elist[:, :], T.zr[:, 0:4], pf(4), A.add)
-    t_pj = cp(T.pf[:, 8:10], T.pj[:, 0:2], w=[t])
     t_xe = tt(T.xe[:, 1:8], T.xa[:, 1:8], T.xb[:, 1:8], A.add, w=[t_xb])
     t_ls = ms(T.land[:, NF:NF + 64], -2.0)
-    ts(col(12), pf(9), 4.0, A.mult, w=[t_pj])
-    t = ts(col(13), pf(9), 0.0625, A.mult)
-    t_te = cp(T.te[:, :], T.xe[:, 0:8].indirect(T.elist[:, 0:4]), w=[t_xe, t_el])
-    ts(col(10), pf(8), 64.0, A.mult, col(12), A.add, w=[t])
-    t = ts(col(11), pf(8), 0.125, A.mult, col(13), A.add)
-    t_bs = act(T.bs[:, :], T.bsi[:, :], None, col(11), 0.015625, w=[t, i_bs])
     ms(T.cum[:, 0:1], 0.0)
-    t_q1 = ts(T.tq1[:, :], T.ti[:, :], col(10), A.add, w=[t, i_ti])
-    t_q0 = ts(T.tq[:, :], T.ti[:, :], col(10), A.add, -0.5, A.add)
-    t_zr = ms(T.zr[:, 8:128], 0.0)
+    t_te = cp(T.te[:, :], T.xe[:, 0:8].indirect(T.elist[:, 0:4]), w=[t_xe, t_el])
+    t_prm = ts(T.prm[:, :], T.pmi[:, :], pf(2), A.add, w=[i_pm])
     t_eq = tt(T.eq[:, :], T.tq1[:, :], T.te[:, :], A.is_equal, w=[t_te, t_q1])
     t2 = tt(T.pq[:, 0:64], T.tq[:, :], T.te[:, :], A.is_ge, w=[t_q0])
     t = tt(T.pq[:, 64:128], T.eq[:, :], T.k8[:, :], A.mult, w=[t_eq, i_k8])
-    t_prm = ts(T.prm[:, :], T.pmi[:, :], pf(2), A.add, w=[i_pm])
-    t = scan(T.cum[:, 1:129], T.pq[:, :], T.zr[:, 0:128], 0.0, A.add, A.add, w=[t, t2, t_zr])
+    t = scan(T.cum[:, 1:129], T.pq[:, :], T.zr[:, 0:128], 0.0, A.add, A.add, w=[t, t2])
     t = tt(T.dif[:, :], T.cum[:, 8:129:8], T.cum[:, 0:128:8], A.subtract, w=[t])
     t = tt(T.off[:, :], T.dif[:, :], T.bs[:, :], A.add, w=[t, t_bs])
     t_lst = ts(T.lst[:, :], T.off[:, :], float(SLOTS), A.mult, w=[t])
 
     MA = ("ma", 14)
-    t_sec = act(T.sec[:, :], T.land[:, 0:NF + 64].indirect(T.lst[:, 8:16]), w=[t_lst, t_ls, t_me, MA])
-    t = tt(T.ym[:, :], T.land[:, 0:NF + 64].indirect(T.lst[:, 0:8]), T.sec[:, :], A.max,
-           w=[MA, t_lst, t_ls, t_me, t_sec])
-    t_zt = tr(T.zt[:, :], T.ym[:, :], w=[t])
+    land = T.land[:, 0:NF + 64]
+    t_a = act(T.sec[:, 0:64], land.indirect(T.lst[:, 8:12]), w=[t_lst, t_ls, t_me, MA])
+    t_b = act(T.sec[:, 64:128], land.indirect(T.lst[:, 12:16]))
+    t_a = tt(T.ym[:, 0:64], land.indirect(T.lst[:, 0:4]), T.sec[:, 0:64], A.max, w=[MA, t_lst, t_ls, t_me, t_a])
+    t_b = tt(T.ym[:, 64:128], land.indirect(T.lst[:, 4:8]), T.sec[:, 64:128], A.max, w=[t_b])
+    tr(T.zt[:, 0:64], T.ym[:, 0:64], w=[t_a])
+    t_zt = tr(T.zt[:, 64:128], T.ym[:, 64:128], w=[t_b])
     t_z0 = cp(T.zf0[:, :], T.zt[:, :].indirect(T.prm[:, 0:4]), w=[t_zt, t_prm])
     t_z1 = act(T.zf1[:, :], T.zt[:, :].indirect(T.prm[:, 4:8]), w=[t_zt, t_prm])
     use("y", t_z0)

@@ -4,16 +4,15 @@ from concourse.mybir import dt, AluOpType, AxisListType, ActivationFunctionType
 SLOTS = 64
 NF = 8 * SLOTS
 NEG = -4194304.0
-WIN = 1800
+WIN = 16192
 
 _SBUF = {
-    "int32": "pi 16 pj 16 raw 64 v 520 g1 32 g2 32",
-    "bfloat16": "mi 128 mb 128 m0 128 m1 128 mn1 128 ml1 128 m5 128 m70 128 m71 128 mki 128 mk 128 c1 32 "
-                "xT 64 x 66 sd0 66 sx 66 uT 32",
+    "int32": "pi 8 raw 64 v 516 g1 32 g2 32",
+    "bfloat16": "mi 130 mb 128 r2 2 m1 128 mn1 128 ml1 128 m5 128 id5 128 mk 128 c1 32 "
+                "xT 96 x 98 sd0 66 sx 66 rl2 32 ct 32 ce 34 zr 128",
     "uint16": "codel 32 voffl 32 slotl 34 gl 32 prm 8 elist 4 lst 16",
-    "float32": "pf 16 cols 16 cwin 96 ctmp 64 zr 128 tf 32 fT 32 fO 32 rl2 32 ct 32 co 32 nz 34 jc 34 nj 34 "
-               "slf 34 vf 32 oh 512 aa 512 bb 512 ohl 16 el1 16 sc 528 win %d exs 4 ex 36 ikc 16 kc 16 cm 16 cs1 16 "
-               "fixc 1 ff 32 cst 32 fr %d land %d ti 64 tq 64 tq1 64 k8 64 bsi 16 bs 16 "
+    "float32": "pf 16 cols 16 cwin 96 ctmp 64 tf 32 vf 32 oh 512 aa 512 bb 512 el1 16 sc 528 win %d exs 4 ex 36 "
+               "kc 16 cm 16 fixc 1 ff 32 cst 32 fr %d land %d ti 64 tq 64 tq1 64 k8 64 bsi 16 bs 16 "
                "pmi 8 xa 8 xb 8 xe 8 te 64 eq 64 pq 128 cum 132 dif 16 off 16 sec 128 ym 128 "
                "zt 128 zf0 64 zf1 64" % (WIN, NF, NF + 64),
 }
@@ -24,7 +23,7 @@ for _d, _s in _SBUF.items():
         SCRATCH[_n] = ("sbuf", [128, int(_w)], _d)
 for _n in ("pa", "pb", "pc", "pd"):
     SCRATCH[_n] = ("psum", [128, 512], "float32")
-SEMAPHORES = ["cv", "cs", "cp", "cg", "ldr", "ldd", "ldv", "exa", "exl", "ma", "ml", "st"]
+SEMAPHORES = ["cv", "cs", "cp", "cg", "ldr", "ldd", "ldv", "fil", "exa", "exl", "ma", "ml", "st"]
 
 
 def rank_program(g, core, T, topo):
@@ -74,9 +73,10 @@ def rank_program(g, core, T, topo):
         use("v", *w)
         return done("v", V.tensor_tensor_scan(out, d0, d1, init, op0, op1))
 
-    def act(out, in_, func=None, bias=0.0, scale=1.0, w=()):
+    def act(out, in_, func=None, bias=0.0, scale=1.0, w=(), accum=None):
         use("s", *w)
-        return done("s", S.activation(out, in_, ACT.Identity if func is None else func, bias=bias, scale=scale))
+        return done("s", S.activation(out, in_, ACT.Identity if func is None else func, bias=bias, scale=scale,
+                                      accum_out=accum))
 
     def mm(out, lhsT, rhs, start, stop, w=()):
         use("p", *w)
@@ -97,68 +97,76 @@ def rank_program(g, core, T, topo):
     S.dma_start(T.raw[:, 48:64], T.dl[1::2, :]).then_inc(T.sem.ldd, 16)
     for w in range(16):
         qq = S if w % 4 == 2 else g.sync
-        qq.dma_start(T.v[w::16, 0:512], T.val[:, :]).then_inc(T.sem.ldv, 16)
+        qq.dma_start(T.v[w::16, 4:516], T.val[:, :]).then_inc(T.sem.ldv, 16)
 
-    t_pi = iota(T.pi[:, 0:1], [[0, 1]], 0, 1, False)
-    i_mb = iota(T.mb[:, :], [[1, 8], [0, 16]], 0, 0)
-    i_mi = iota(T.mi[:, :], [[1, 128]], 0, 0)
-    i_mk = iota(T.mki[0:1, :], [[0, 4], [1, 32]], 0, 0)
-
-    t_sd = ms(T.sd0[:, 0:65], 1.0)
-    t_win0 = ms(T.win[:, 512:640], -2.0)
     p0 = T.pi[:, 0:1]
-    ts(T.pi[:, 5:6], p0, 4, A.logical_shift_right, w=[t_pi])
+    t_pi = iota(p0, [[0, 1]], 0, 1, False)
+    i_mi = iota(T.mi[:, 0:130], [[1, 130]], -1, 0)
+    i_mb = iota(T.mb[:, :], [[1, 8], [0, 16]], 0, 0)
+    i_v = iota(T.v[:, 0:4], [[1, 2], [0, 2]], -2, 0, False)
+    m32 = T.mi[:, 1:33]
+
+    t_mk = ms(T.mk[0:1, :], 0.0)
+    t_sd = ms(T.sd0[:, 0:65], 1.0)
+    t_w0 = ms(T.win[:, 448:576], -2.0)
+    use("y", t_w0)
+    for a in (64, 192, 320):
+        g.sync.dma_start(T.win[:, a:a + 128], T.win[:, 448:576]).then_inc(T.sem.fil, 16)
+    FIL = ("fil", 48)
+    t_sd = act(T.sd0[:, 32:33], T.win[:, 448:449], None, 0.0, 0.0, w=[t_w0, t_sd])
+    t_mk = act(T.mk[0:1, 0:128:32], T.win[0:1, 448:452], None, 16.0, 0.0, w=[t_mk])
+    t_cum = act(T.cum[:, 0:1], T.win[:, 448:449], None, 0.0, 0.0)
+    act(T.sc[:, 0:1], T.win[:, 448:449], None, -2.0, 0.0)
+    t_sc0 = act(T.sc[:, 513:528], T.win[:, 448:463], None, -2.0, 0.0)
+    t_zr = act(T.zr[:, :], T.win[:, 448:576], None, 0.0, 0.0)
+    ts(T.pi[:, 3:4], p0, 3, A.logical_shift_right, 1, A.bitwise_and, w=[t_pi])
+    ts(T.pi[:, 5:6], p0, 4, A.logical_shift_right)
     ts(T.pi[:, 1:2], p0, 31, A.bitwise_and)
-    ts(T.pi[:, 2:3], p0, 15, A.bitwise_and)
-    ts(T.pi[:, 3:4], p0, 3, A.logical_shift_right, 1, A.bitwise_and)
+    ts(T.pi[:, 2:3], p0, 1, A.bitwise_and)
     t = ts(T.pi[:, 4:5], p0, 7, A.bitwise_and)
-    t_sd = ms(T.sd0[:, 32:33], 0.0, w=[t_sd])
     t_pf = cp(T.pf[:, 0:6], T.pi[:, 0:6], w=[t])
-    t_mn = ts(T.mn1[:, :], T.mb[:, :], pf(5), A.is_equal, -1.0, A.mult, w=[i_mb, t_pf])
-    ts(col(1), pf(1), 31.0, A.not_equal)
-    t_c3 = ts(col(3), pf(0), 1.0, A.add)
-    ts(col(0), pf(1), 31.0, A.is_equal)
-    t_c2 = ts(col(2), pf(5), -1.0, A.add)
-    t_x1 = ts(T.x[:, 64:65], pf(2), 0.0, A.is_equal)
-    t_m1 = ts(T.m1[:, :], T.mb[:, :], pf(5), A.is_equal)
-    t_m5 = ts(T.m5[:, :], T.mi[:, :], col(3), A.is_equal, col(1), A.mult, w=[i_mi, t_c3])
-    ts(T.m70[:, :], T.mb[:, :], col(2), A.is_equal, col(0), A.mult, w=[t_c2])
-    t_m7 = ts(T.m71[:, :], T.mb[:, :], pf(5), A.is_equal, col(0), A.mult)
-    t_m0 = ts(T.m0[:, :], T.m1[:, :], T.x[:, 64:65], A.mult, w=[t_m1])
 
     t_c7 = act(col(7), pf(4), None, pf(3), 2.0, w=[t_pf])
-    act(T.cwin[:, 32:64], T.mi[:, 0:32], None, -2.0, 2097152.0, w=[i_mi])
-    t_cb = act(T.ctmp[:, 0:32], T.mi[:, 0:32], ACT.Abs, col(7), -1.0, w=[t_c7])
-    t_mk = act(T.mk[0:1, :], T.mki[0:1, :], ACT.Relu, 16.0, -16.0, w=[i_mk])
-    t_cw = act(T.cwin[:, 0:32], T.ctmp[:, 0:32], None, 0.0, NEG, w=[t_cb])
-    for a in (384, 256, 128):
-        act(T.win[:, a:a + 128], T.win[:, 512:640], w=[t_win0])
-
-    use("g", t_mn)
-    t_l = done("g", g.affine_select(T.ml1[:, :], T.mn1[:, :], [[-1, 128]], A.is_gt, 0.0, 0, 1))
-    i_jc = iota(T.jc[:, 0:33], [[16, 33]], 577, 1)
-    i_v = iota(T.v[:, 512:520], [[-1, 8]], 1, 0, False)
-
+    t_c1c = act(col(1), pf(1), ACT.Sign, 31.0, -1.0)
+    t_p6 = act(pf(6), pf(5), None, pf(0), -16.0)
     t_tf = cp(T.tf[:, :], T.raw[:, 0:32], w=[LDR])
     t_rl2 = ts(T.rl2[:, :], T.raw[:, 0:32], 2.0, A.is_equal)
-    ts(T.xT[:, 32:64], T.raw[:, 0:32], 0.0, A.is_equal)
-    t_xT = ts(T.xT[:, 0:32], T.raw[:, 32:64], 2.0, A.is_equal, w=[LDD])
+    t_hd = act(T.xT[:, 64:96], T.tf[:, :], ACT.Relu, 1.0, -1.0, w=[t_tf])
+    act(T.cwin[:, 32:64], m32, None, -2.0, 2097152.0, w=[i_mi])
+    t_cb = act(T.ctmp[:, 0:32], m32, ACT.Abs, col(7), -1.0, w=[t_c7])
+    t_sg = act(col(2), pf(6), ACT.Sign, w=[t_p6])
+    t_cw = act(T.cwin[:, 0:32], T.ctmp[:, 0:32], None, 0.0, NEG, w=[t_cb])
+    t_x1 = act(T.x[:, 96:97], col(2), None, 1.0, -1.0, w=[t_sg])
+    t_c4 = act(col(4), col(2), None, 1.0, -1.0)
+    t_c3 = act(col(3), pf(6), ACT.Relu, 14.0 * NEG, -NEG)
+    t_ext = act(T.ce[:, 32:33], col(2), None, pf(6), 15.0)
+
     t_c1 = scan(T.c1[:, :], T.rl2[:, :], T.tf[:, :], 0.0, A.mult, A.add, w=[t_rl2])
-    t_x = tr(T.x[:, 0:64], T.xT[:, :], w=[t_xT])
-    t_uT = ts(T.uT[:, :], T.raw[:, 32:64], 2.0, A.is_lt, 516.0, A.mult)
-    mm(T.pa[:, 0:2], T.mk[0:1, :], T.m1[0:1, 0:2], True, False, w=[t_mk, t_m1])
+    t_m5 = ts(T.m5[:, :], T.mi[:, 0:128], pf(0), A.is_equal, col(1), A.mult, w=[i_mi, t_c1c])
+    ts(T.xT[:, 32:64], T.raw[:, 32:64], 2.0, A.is_equal, w=[LDD])
+    t_xT = ts(T.xT[:, 0:32], T.raw[:, 32:64], 600.0, A.mult, -600.0, A.add)
+    t_mn = ts(T.mn1[:, :], T.mb[:, :], pf(5), A.is_equal, -1.0, A.mult, w=[i_mb])
+    use("g", t_mn)
+    t_l = done("g", g.affine_select(T.ml1[:, :], T.mn1[:, :], [[-1, 128]], A.is_gt, 0.0, 0, 1))
+    mm(T.pa[:, 0:2], T.mk[0:1, :], T.sd0[0:1, 0:2], True, False, w=[t_mk, t_sd])
     t_pa = mm(T.pa[:, 0:2], T.m5[:, :], T.c1[:, 15:32:16], False, True, w=[t_c1, t_m5])
-    t_sx = scan(T.sx[:, 0:65], T.sd0[:, 0:65], T.x[:, 0:65], 0.0, A.mult, A.add, w=[t_x, t_sd, t_x1])
+    t_x = tr(T.x[:, 0:96], T.xT[:, :], w=[t_xT, t_hd])
+    act(T.r2[:, 1:2], T.x[:, 64:65], None, 0.0, col(4), w=[t_x, t_c4])
     scan(T.ct[:, 0:16], T.rl2[:, 0:16], T.tf[:, 0:16], T.pa[:, 0:1], A.mult, A.add, w=[t_pa])
     t_ct = scan(T.ct[:, 16:32], T.rl2[:, 16:32], T.tf[:, 16:32], T.pa[:, 1:2], A.mult, A.add)
-    mm(T.pb[:, 1:2], T.m70[:, :], T.c1[:, 15:16], True, False, w=[t_m7])
-    mm(T.pb[:, 1:2], T.m71[:, :], T.c1[:, 31:32], False, True)
-    mm(T.pb[:, 2:3], T.m0[:, :], T.x[:, 32:33], True, True, w=[t_x, t_m0])
-    t_pb = mm(T.pb[:, 0:1], T.m1[:, :], T.sx[:, 63:64], True, True, w=[t_sx])
-    mm(T.pd[:, 0:32], T.ml1[:, :], T.x[:, 0:32], True, False, w=[t_l])
+    t_sx = scan(T.sx[:, 0:65], T.sd0[:, 0:65], T.x[:, 32:97], 0.0, A.mult, A.add, w=[t_x, t_sd, t_x1])
+    t_co = tr(T.ce[:, 0:32], T.ct[:, :], w=[t_ct])
+    t_r2 = act(T.r2[:, 0:1], T.ce[:, 31:32], None, 0.0, col(3), w=[t_co, t_c3])
+    t_m1 = ts(T.m1[:, :], T.mb[:, :], pf(5), A.is_equal)
+    t_code = cp(T.codel[:, :], T.ce[:, 0:32], w=[t_co])
+    t_id = ts(T.id5[:, :], T.mi[:, 1:129], pf(0), A.is_equal, 520.0, A.mult)
+    mm(T.pb[:, 0:1], T.m1[:, :], T.sx[:, 63:64], True, True, w=[t_sx, t_m1])
+    mm(T.pd[:, 0:32], T.ml1[:, :], T.x[:, 32:64], True, False, w=[t_l])
     t_pd = mm(T.pd[:, 0:32], T.m1[:, :], T.sx[:, 0:32], False, True)
-    mm(T.pc[:, 0:33], T.ml1[:, :], T.x[:, 32:65], True, False, w=[t_x1])
-    t_pc = mm(T.pc[:, 0:33], T.m1[:, :], T.sx[:, 32:65], False, True)
+    t_pb = mm(T.pb[:, 1:3], T.m1[:, :], T.r2[:, 0:2], True, True, w=[t_r2])
+    mm(T.pc[:, 0:33], T.ml1[:, :], T.x[:, 64:97], True, False, w=[t_x1])
+    mm(T.pc[:, 0:33], T.m1[:, :], T.sx[:, 32:65], False, False)
+    t_pc = mm(T.pc[:, 0:33], T.id5[:, :], T.ce[:, 0:33], False, True, w=[t_id, t_co, t_ext])
 
     others = [c for c in T.cores if c != core]
 
@@ -172,10 +180,8 @@ def rank_program(g, core, T, topo):
             m &= topo.mask(src, c)
         return m
 
-    t_fT = tt(T.fT[:, :], T.uT[:, :], T.raw[:, 32:64], A.subtract, w=[t_uT])
+    t_vf = tt(T.vf[:, :], T.pd[:, 0:32], T.x[:, 0:32], A.min, w=[t_pd])
     t_exs = cp(T.exs[:, 0:3], T.pb[:, 0:3], w=[t_pb])
-    t_co = tr(T.co[:, :], T.ct[:, :], w=[t_ct])
-    t_fO = tr(T.fO[:, :], T.fT[:, :], w=[t_fT])
     use("g", t_exs)
     o = 4 * (q + 1)
     g.remote_dma_fused([RemoteDMATransfer(dst_ids=[dst_id(c) for c in others],
@@ -183,72 +189,55 @@ def rank_program(g, core, T, topo):
                                           src=T.exs[:, 0:2], dsts=[T.ex[:, o:o + 2] for _ in others])],
                        local_sem=T.sem.exl)
     EXA = ("exa", sum(bin(common(c, [d for d in T.cores if d != c])).count("1") for c in others))
-    i_zr = iota(T.zr[:, :], [[0, 128]], 0, 0)
-    i_ff = iota(T.ff[:, :], [[8, 8], [128, 4]], 0, 0)
-    i_kc = iota(T.ikc[:, :], [[-2, 16]], -2, 0)
+    i_ff = iota(T.ff[:, :], [[8, 8], [128, 4]], 1, 0)
     i_ti = iota(T.ti[:, :], [[1, 4], [512, 2], [0, 8]], 8 * q, 0)
-    i_k8 = iota(T.k8[:, :], [[0, 8], [1, 8]], -8, 0)
     i_bs = iota(T.bsi[:, :], [[512, 2], [1, 4], [0, 2]], 0, 0)
-    i_pm = iota(T.pmi[:, :], [[16, 2], [32, 4]], 0, 0)
+    i_k8 = iota(T.k8[:, :], [[0, 8], [1, 8]], -8, 0)
 
-    t_code = cp(T.codel[:, :], T.co[:, :], w=[t_co])
     t_oh0 = act(T.oh[:, 0:256], T.cwin[:, 0:32].indirect(T.codel[:, 0:16]), w=[t_code, t_cw])
     t_oh1 = act(T.oh[:, 256:512], T.cwin[:, 0:32].indirect(T.codel[:, 16:32]))
     t_aa0 = act(T.aa[:, 0:256], T.cwin[:, 32:64].indirect(T.codel[:, 0:16]))
     t_aa1 = act(T.aa[:, 256:512], T.cwin[:, 32:64].indirect(T.codel[:, 16:32]))
-    t_win = act(T.win[:, 64:128], T.win[:, 512:576])
-    t = tt(T.vf[:, :], T.pd[:, 0:32], T.fO[:, :], A.max, w=[t_pd, t_fO])
-    t_nz = ts(T.nz[:, 0:33], T.x[:, 32:65], 0.0, A.is_equal)
-    t_voff = ts(T.voffl[:, :], T.vf[:, :], -1.0, A.add, w=[t])
-    t_nj = tt(T.nj[:, 0:33], T.nz[:, 0:33], T.jc[:, 0:33], A.mult, w=[t_nz, i_jc])
-    ts(T.pj[:, 0:1], p0, 1, A.logical_shift_right, 7, A.bitwise_and)
-    t = ts(T.pj[:, 1:2], p0, 1, A.bitwise_and)
-    ms(T.sc[:, 0:1], -2.0)
-    t_pj = cp(T.pf[:, 8:10], T.pj[:, 0:2], w=[t])
+    t_voff = ts(T.voffl[:, :], T.vf[:, :], 3.0, A.add, w=[t_vf])
+    t_slot = ts(T.slotl[:, 0:33], T.pc[:, 0:33], T.exs[:, 2:3], A.subtract, 63.0, A.add, w=[t_pc, t_exs])
 
-    t_b0 = tt(T.bb[:, 0:256], T.v[:, 0:520].indirect(T.voffl[:, 0:16]), T.oh[:, 0:256], A.add,
-              w=[LDV, i_v, t_voff, t_oh0])
-    t_slf = tt(T.slf[:, 0:33], T.pc[:, 0:33], T.nj[:, 0:33], A.add, w=[t_pc, t_nj])
-    t_b1 = tt(T.bb[:, 256:512], T.v[:, 0:520].indirect(T.voffl[:, 16:32]), T.oh[:, 256:512], A.add, w=[t_oh1])
-    t_slot = ts(T.slotl[:, 0:33], T.slf[:, 0:33], 63.0, A.add, w=[t_slf])
-    t = scan(T.sc[:, 1:257], T.aa[:, 0:256], T.bb[:, 0:256], -2.0, A.min, A.max, w=[t_b0, t_aa0])
-    t_sc0 = ms(T.sc[:, 513:528], -2.0)
+    vw = T.v[:, 0:516]
+    t_b0 = tt(T.bb[:, 0:256], vw.indirect(T.voffl[:, 0:16]), T.oh[:, 0:256], A.add, w=[LDV, i_v, t_voff, t_oh0])
+    t_b1 = tt(T.bb[:, 256:512], vw.indirect(T.voffl[:, 16:32]), T.oh[:, 256:512], A.add, w=[t_oh1])
+    t = scan(T.sc[:, 1:257], T.aa[:, 0:256], T.bb[:, 0:256], -2.0, A.min, A.max, w=[t_b0, t_aa0, t_sc0])
     t = scan(T.sc[:, 257:513], T.aa[:, 256:512], T.bb[:, 256:512], T.sc[:, 256:257], A.min, A.max,
              w=[t_b1, t_aa1, t])
-    t_scat = cp(T.win[:, 0:WIN].indirect(T.slotl[:, 0:33]), T.sc[:, :], w=[t, t_slot, t_sc0, t_win0, t_win])
+    t_scat = cp(T.win[:, 0:WIN].indirect(T.slotl[:, 0:33]), T.sc[:, :], w=[t, t_slot, t_sc0, t_w0, FIL])
 
-    t_c9 = act(col(9), pf(3), None, pf(4), 64.0)
-    t_ca = act(T.ctmp[:, 32:64], T.mi[:, 0:32], ACT.Relu, 16.0, -1.0)
     t_own = act(T.ex[:, o:o + 2], T.exs[:, 0:2], w=[t_exs])
-    t_cw = act(T.cwin[:, 64:96], T.ctmp[:, 32:64], None, 0.0, NEG, w=[t_ca])
+    t_cb = act(col(8), col(7), None, -16.0 * NEG, -NEG)
+    t_c9 = act(col(9), pf(3), None, pf(4), 64.0)
+    act(T.cwin[:, 64:80], T.mi[:, 1:17], None, -64.0 * NEG, 0.0)
+    t_w = act(T.cwin[:, 80:96], T.mi[:, 17:33], None, col(8), NEG, w=[t_cb])
     t_cst = act(T.cst[:, :], T.ff[:, :], None, col(9), w=[i_ff, t_c9])
-    t_ohl = act(T.ohl[:, :], T.cwin[:, 64:96].indirect(T.codel[:, 0:1]), w=[t_cw])
-    t_kc = act(T.kc[:, :], T.ikc[:, :], None, col(7), w=[i_kc])
-    act(col(12), pf(9), None, 0.0, 4.0, w=[t_pj])
-    t = act(col(13), pf(9), None, 0.0, 0.0625)
-    act(col(10), pf(8), None, col(12), 64.0, w=[t])
-    t_c11 = act(col(11), pf(8), None, col(13), 0.125)
+    if q:
+        t_kc = act(T.kc[:, :], T.cwin[:, 64:96].indirect(T.codel[:, 0:1]), w=[t_w])
+    t = act(col(12), pf(2), None, 0.0, -28.0)
+    act(col(11), pf(6), None, 0.0, 0.0625)
+    t_c11 = act(col(10), pf(6), None, col(12), 32.0, w=[t])
 
     if q:
-        t_el = tt(T.el1[:, :], T.v[:, 0:520].indirect(T.voffl[:, 0:1]), T.ohl[:, :], A.add, w=[t_ohl])
-    t_xa = scan(T.xa[:, 1:8], T.ex[:, 4:32:4], T.zr[:, 0:7], -1.0, A.add, A.add, w=[EXA, t_own, i_zr])
-    if q:
-        t_cm = ts(T.cm[:, :], T.kc[:, :], T.ex[:, 4 * q + 1:4 * q + 2], A.not_equal, NEG, A.mult, w=[t_kc])
-        t_g1 = ts(T.g1[:, :], T.cst[:, :], T.xa[:, q:q + 1], A.subtract, T.exs[:, 2:3], A.subtract,
-                  w=[t_xa, t_cst])
-        t_cs1 = tt(T.cs1[:, 0:15], T.cm[:, 0:15], T.el1[:, 0:15], A.add, w=[t_cm, t_el])
-    else:
-        t_g1 = ts(T.g1[:, :], T.cst[:, :], 1.0, A.add, T.exs[:, 2:3], A.subtract, w=[t_cst])
-    t_g2 = ts(T.g2[:, :], T.g1[:, :], NF - 1, A.bitwise_and, w=[t_g1])
-    t_fix = t_scat
-    if q:
-        use("v", t_cs1)
-        t = done("v", V.tensor_reduce(T.fixc[:, :], T.cs1[:, 0:15], AxisListType.X, A.max))
-    t_gl = ts(T.gl[:, :], T.g2[:, :], T.exs[:, 2:3], A.add, w=[t_g2])
-    if q:
+        t_nb = act(T.ctmp[:, 32:32 + q], T.ex[:, 4:4 + 4 * q:4], None, 0.0, -1.0, w=[EXA], accum=col(14))
+        t_cm = act(T.cm[:, :], T.kc[:, :], ACT.Abs, T.ex[:, 4 * q + 1:4 * q + 2], -1.0, w=[t_kc])
+        t_g1 = ts(T.g1[:, :], T.cst[:, :], col(14), A.add, T.exs[:, 2:3], A.subtract, w=[t_nb, t_cst])
+        t_el = tt(T.el1[:, :], vw.indirect(T.voffl[:, 0:1]), T.cm[:, :], A.subtract, w=[t_cm])
+        t_g2 = ts(T.g2[:, :], T.g1[:, :], NF - 1, A.bitwise_and, w=[t_g1])
+        use("v", t_el)
+        t = done("v", V.tensor_reduce(T.fixc[:, :], T.el1[:, :], AxisListType.X, A.max))
+        t_gl = cp(T.gl[:, :], T.g2[:, :], w=[t_g2])
         t_fix = tt(T.win[:, 64:65], T.win[:, 64:65], T.fixc[:, :], A.max, w=[t, t_scat])
-    t_f0 = cp(T.fr[:, 0:256], T.win[:, 64:640].indirect(T.gl[:, 0:16]), w=[t_gl, t_fix])
-    t_f1 = act(T.fr[:, 256:512], T.win[:, 64:640].indirect(T.gl[:, 16:32]), w=[t_gl, t_fix])
+    else:
+        t_g1 = ts(T.g1[:, :], T.cst[:, :], T.exs[:, 2:3], A.subtract, w=[t_cst])
+        t_g2 = ts(T.g2[:, :], T.g1[:, :], NF - 1, A.bitwise_and, w=[t_g1])
+        t_gl = cp(T.gl[:, :], T.g2[:, :], w=[t_g2])
+        t_fix = t_scat
+    t_f0 = cp(T.fr[:, 0:256], T.win[:, 64:576].indirect(T.gl[:, 0:16]), w=[t_gl, t_fix])
+    t_f1 = act(T.fr[:, 256:512], T.win[:, 64:576].indirect(T.gl[:, 16:32]), w=[t_gl, t_fix])
 
     near = [d for d in range(8) if d != q and topo.die(T.cores[d]) == topo.die(core)]
     far = [d for d in range(8) if d != q and topo.die(T.cores[d]) != topo.die(core)]
@@ -266,32 +255,33 @@ def rank_program(g, core, T, topo):
         k += 4
     use("g", t_f0, t_f1)
     g.remote_dma_fused(trs, local_sem=T.sem.ml)
+    i_ls = iota(T.land[:, NF:NF + 64], [[0, 64]], -2, 0)
+    i_pm = iota(T.pmi[:, :], [[16, 2], [32, 4]], 0, 0)
 
     t_q1 = act(T.tq1[:, :], T.ti[:, :], None, col(10), w=[t_c11, i_ti])
     t_q0 = act(T.tq[:, :], T.tq1[:, :], None, -0.5, w=[t_q1])
     t_bs = act(T.bs[:, :], T.bsi[:, :], None, col(11), 0.015625, w=[i_bs])
     t_me = act(T.land[:, SLOTS * q:SLOTS * q + SLOTS], T.fr[:, SLOTS * q:SLOTS * q + SLOTS], w=[t_f0, t_f1])
+    t_xa = scan(T.xa[:, 1:8], T.ex[:, 4:32:4], T.zr[:, 0:7], -1.0, A.add, A.add, w=[EXA, t_own, t_zr])
     t_xb = ts(T.xb[:, 1:8], T.ex[:, 8:36:4], 512.0, A.is_ge, 0.25, A.mult)
     ts(T.xe[:, 0:1], T.xa[:, 7:8], T.ex[:, 32:33], A.add, 0.25, A.add, w=[t_xa, EXA])
     t_el = ts(T.elist[:, :], T.zr[:, 0:4], pf(4), A.add)
     t_xe = tt(T.xe[:, 1:8], T.xa[:, 1:8], T.xb[:, 1:8], A.add, w=[t_xb])
-    t_ls = ms(T.land[:, NF:NF + 64], -2.0)
-    ms(T.cum[:, 0:1], 0.0)
     t_te = cp(T.te[:, :], T.xe[:, 0:8].indirect(T.elist[:, 0:4]), w=[t_xe, t_el])
-    t_prm = ts(T.prm[:, :], T.pmi[:, :], pf(2), A.add, w=[i_pm])
     t_eq = tt(T.eq[:, :], T.tq1[:, :], T.te[:, :], A.is_equal, w=[t_te, t_q1])
     t2 = tt(T.pq[:, 0:64], T.tq[:, :], T.te[:, :], A.is_ge, w=[t_q0])
     t = tt(T.pq[:, 64:128], T.eq[:, :], T.k8[:, :], A.mult, w=[t_eq, i_k8])
-    t = scan(T.cum[:, 1:129], T.pq[:, :], T.zr[:, 0:128], 0.0, A.add, A.add, w=[t, t2])
+    t = scan(T.cum[:, 1:129], T.pq[:, :], T.zr[:, 0:128], 0.0, A.add, A.add, w=[t, t2, t_cum])
     t = tt(T.dif[:, :], T.cum[:, 8:129:8], T.cum[:, 0:128:8], A.subtract, w=[t])
     t = tt(T.off[:, :], T.dif[:, :], T.bs[:, :], A.add, w=[t, t_bs])
     t_lst = ts(T.lst[:, :], T.off[:, :], float(SLOTS), A.mult, w=[t])
+    t_prm = ts(T.prm[:, :], T.pmi[:, :], pf(6), A.add, w=[i_pm])
 
     MA = ("ma", 14)
     land = T.land[:, 0:NF + 64]
-    t_a = act(T.sec[:, 0:64], land.indirect(T.lst[:, 8:12]), w=[t_lst, t_ls, t_me, MA])
+    t_a = act(T.sec[:, 0:64], land.indirect(T.lst[:, 8:12]), w=[t_lst, i_ls, t_me, MA])
     t_b = act(T.sec[:, 64:128], land.indirect(T.lst[:, 12:16]))
-    t_a = tt(T.ym[:, 0:64], land.indirect(T.lst[:, 0:4]), T.sec[:, 0:64], A.max, w=[MA, t_lst, t_ls, t_me, t_a])
+    t_a = tt(T.ym[:, 0:64], land.indirect(T.lst[:, 0:4]), T.sec[:, 0:64], A.max, w=[MA, t_lst, i_ls, t_me, t_a])
     t_b = tt(T.ym[:, 64:128], land.indirect(T.lst[:, 4:8]), T.sec[:, 64:128], A.max, w=[t_b])
     tr(T.zt[:, 0:64], T.ym[:, 0:64], w=[t_a])
     t_zt = tr(T.zt[:, 64:128], T.ym[:, 64:128], w=[t_b])
@@ -305,4 +295,4 @@ def rank_program(g, core, T, topo):
     use("y", ("st", 32))
     for k in ("v", "s", "p", "g"):
         use("g", ("c" + k, cnt[k]))
-    use("g", ("exl", bin(common(core, others)).count("1")), ("ml", 14), EXA)
+    use("g", ("exl", bin(common(core, others)).count("1")), ("ml", 14), EXA, FIL, LDR, LDD, LDV)

from concourse.bass import DstId, RemoteDMATransfer
from concourse.mybir import dt, AluOpType, AxisListType, ActivationFunctionType

SLOTS = 64
NF = 8 * SLOTS
NEG = -4194304.0
WIN = 16192

_SBUF = {
    "int32": "pi 8 raw 64 v 516 g1 32 g2 32",
    "bfloat16": "mi 130 mb 128 r2 2 m1 128 mn1 128 ml1 128 m5 128 id5 128 mk 128 c1 32 "
                "xT 96 x 98 sd0 66 sx 66 rl2 32 ct 32 ce 34 zr 128",
    "uint16": "codel 32 voffl 32 slotl 34 gl 32 prm 8 elist 4 lst 16",
    "float32": "pf 16 cols 16 cwin 96 ctmp 64 tf 32 vf 32 oh 512 aa 512 bb 512 el1 16 sc 528 win %d exs 4 ex 36 "
               "kc 16 cm 16 fixc 1 ff 32 cst 32 fr %d land %d ti 64 tq 64 tq1 64 k8 64 bsi 16 bs 16 "
               "pmi 8 xa 8 xb 8 xe 8 te 64 eq 64 pq 128 cum 132 dif 16 off 16 sec 128 ym 128 "
               "zt 128 zf0 64 zf1 64" % (WIN, NF, NF + 64),
}
SCRATCH = {}
for _d, _s in _SBUF.items():
    _s = _s.split()
    for _n, _w in zip(_s[0::2], _s[1::2]):
        SCRATCH[_n] = ("sbuf", [128, int(_w)], _d)
for _n in ("pa", "pb", "pc", "pd"):
    SCRATCH[_n] = ("psum", [128, 512], "float32")
SEMAPHORES = ["cv", "cs", "cp", "cg", "ldr", "ldd", "ldv", "fil", "exa", "exl", "ma", "ml", "st"]


def rank_program(g, core, T, topo):
    q = T.rank_of(core)
    if q is None:
        return
    A, ACT = AluOpType, ActivationFunctionType
    V, S, P = g.vector, g.scalar, g.tensor
    queues = {"v": V, "s": S, "p": P, "g": g, "y": g.sync}
    cnt = {k: 0 for k in queues}
    known = {k: {} for k in queues}

    def use(k, *toks):
        for sem, val in toks:
            if known[k].get(sem, 0) < val:
                queues[k].wait_ge(T.sem[sem], val)
                known[k][sem] = val

    def done(k, ins):
        cnt[k] += 1
        ins.then_inc(T.sem["c" + k], 1)
        return ("c" + k, cnt[k])

    def ts(out, in0, s1, op0, s2=None, op1=None, w=()):
        use("v", *w)
        if op1 is None:
            return done("v", V.tensor_scalar(out, in0, s1, None, op0))
        return done("v", V.tensor_scalar(out, in0, s1, s2, op0, op1))

    def tt(out, a, b, op, w=()):
        use("v", *w)
        return done("v", V.tensor_tensor(out, a, b, op))

    def cp(out, in_, w=()):
        use("v", *w)
        return done("v", V.tensor_copy(out, in_))

    def ms(ap, c, w=()):
        use("v", *w)
        return done("v", V.memset(ap, c))

    def tr(out, in_, w=()):
        use("v", *w)
        return done("v", V.transpose(out, in_))

    def scan(out, d0, d1, init, op0, op1, w=()):
        use("v", *w)
        return done("v", V.tensor_tensor_scan(out, d0, d1, init, op0, op1))

    def act(out, in_, func=None, bias=0.0, scale=1.0, w=(), accum=None):
        use("s", *w)
        return done("s", S.activation(out, in_, ACT.Identity if func is None else func, bias=bias, scale=scale,
                                      accum_out=accum))

    def mm(out, lhsT, rhs, start, stop, w=()):
        use("p", *w)
        return done("p", P.matmul(out, lhsT, rhs, start, stop))

    def iota(out, pattern, base, mult, flag=True):
        if not flag:
            return done("g", g.iota(out, pattern, base, mult))
        return done("g", g.iota(out, pattern, base, mult, allow_small_or_imprecise_dtypes=True))

    pf = lambda k: T.pf[:, k:k + 1]
    col = lambda k: T.cols[:, k:k + 1]

    LDR, LDD, LDV = ("ldr", 32), ("ldd", 32), ("ldv", 256)
    g.sync.dma_start(T.raw[:, 0:16], T.rl[0::2, :]).then_inc(T.sem.ldr, 16)
    S.dma_start(T.raw[:, 16:32], T.rl[1::2, :]).then_inc(T.sem.ldr, 16)
    g.sync.dma_start(T.raw[:, 32:48], T.dl[0::2, :]).then_inc(T.sem.ldd, 16)
    S.dma_start(T.raw[:, 48:64], T.dl[1::2, :]).then_inc(T.sem.ldd, 16)
    for w in range(16):
        qq = S if w % 4 == 2 else g.sync
        qq.dma_start(T.v[w::16, 4:516], T.val[:, :]).then_inc(T.sem.ldv, 16)

    p0 = T.pi[:, 0:1]
    t_pi = iota(p0, [[0, 1]], 0, 1, False)
    i_mi = iota(T.mi[:, 0:130], [[1, 130]], -1, 0)
    i_mb = iota(T.mb[:, :], [[1, 8], [0, 16]], 0, 0)
    i_v = iota(T.v[:, 0:4], [[1, 2], [0, 2]], -2, 0, False)
    m32 = T.mi[:, 1:33]

    t_mk = ms(T.mk[0:1, :], 0.0)
    t_sd = ms(T.sd0[:, 0:65], 1.0)
    t_w0 = ms(T.win[:, 448:576], -2.0)
    use("y", t_w0)
    for a in (64, 192, 320):
        g.sync.dma_start(T.win[:, a:a + 128], T.win[:, 448:576]).then_inc(T.sem.fil, 16)
    FIL = ("fil", 48)
    t_sd = act(T.sd0[:, 32:33], T.win[:, 448:449], None, 0.0, 0.0, w=[t_w0, t_sd])
    t_mk = act(T.mk[0:1, 0:128:32], T.win[0:1, 448:452], None, 16.0, 0.0, w=[t_mk])
    t_cum = act(T.cum[:, 0:1], T.win[:, 448:449], None, 0.0, 0.0)
    act(T.sc[:, 0:1], T.win[:, 448:449], None, -2.0, 0.0)
    t_sc0 = act(T.sc[:, 513:528], T.win[:, 448:463], None, -2.0, 0.0)
    t_zr = act(T.zr[:, :], T.win[:, 448:576], None, 0.0, 0.0)
    ts(T.pi[:, 3:4], p0, 3, A.logical_shift_right, 1, A.bitwise_and, w=[t_pi])
    ts(T.pi[:, 5:6], p0, 4, A.logical_shift_right)
    ts(T.pi[:, 1:2], p0, 31, A.bitwise_and)
    ts(T.pi[:, 2:3], p0, 1, A.bitwise_and)
    t = ts(T.pi[:, 4:5], p0, 7, A.bitwise_and)
    t_pf = cp(T.pf[:, 0:6], T.pi[:, 0:6], w=[t])

    t_c7 = act(col(7), pf(4), None, pf(3), 2.0, w=[t_pf])
    t_c1c = act(col(1), pf(1), ACT.Sign, 31.0, -1.0)
    t_p6 = act(pf(6), pf(5), None, pf(0), -16.0)
    t_tf = cp(T.tf[:, :], T.raw[:, 0:32], w=[LDR])
    t_rl2 = ts(T.rl2[:, :], T.raw[:, 0:32], 2.0, A.is_equal)
    t_hd = act(T.xT[:, 64:96], T.tf[:, :], ACT.Relu, 1.0, -1.0, w=[t_tf])
    act(T.cwin[:, 32:64], m32, None, -2.0, 2097152.0, w=[i_mi])
    t_cb = act(T.ctmp[:, 0:32], m32, ACT.Abs, col(7), -1.0, w=[t_c7])
    t_sg = act(col(2), pf(6), ACT.Sign, w=[t_p6])
    t_cw = act(T.cwin[:, 0:32], T.ctmp[:, 0:32], None, 0.0, NEG, w=[t_cb])
    t_x1 = act(T.x[:, 96:97], col(2), None, 1.0, -1.0, w=[t_sg])
    t_c4 = act(col(4), col(2), None, 1.0, -1.0)
    t_c3 = act(col(3), pf(6), ACT.Relu, 14.0 * NEG, -NEG)
    t_ext = act(T.ce[:, 32:33], col(2), None, pf(6), 15.0)

    t_c1 = scan(T.c1[:, :], T.rl2[:, :], T.tf[:, :], 0.0, A.mult, A.add, w=[t_rl2])
    t_m5 = ts(T.m5[:, :], T.mi[:, 0:128], pf(0), A.is_equal, col(1), A.mult, w=[i_mi, t_c1c])
    ts(T.xT[:, 32:64], T.raw[:, 32:64], 2.0, A.is_equal, w=[LDD])
    t_xT = ts(T.xT[:, 0:32], T.raw[:, 32:64], 600.0, A.mult, -600.0, A.add)
    t_mn = ts(T.mn1[:, :], T.mb[:, :], pf(5), A.is_equal, -1.0, A.mult, w=[i_mb])
    use("g", t_mn)
    t_l = done("g", g.affine_select(T.ml1[:, :], T.mn1[:, :], [[-1, 128]], A.is_gt, 0.0, 0, 1))
    mm(T.pa[:, 0:2], T.mk[0:1, :], T.sd0[0:1, 0:2], True, False, w=[t_mk, t_sd])
    t_pa = mm(T.pa[:, 0:2], T.m5[:, :], T.c1[:, 15:32:16], False, True, w=[t_c1, t_m5])
    t_x = tr(T.x[:, 0:96], T.xT[:, :], w=[t_xT, t_hd])
    act(T.r2[:, 1:2], T.x[:, 64:65], None, 0.0, col(4), w=[t_x, t_c4])
    scan(T.ct[:, 0:16], T.rl2[:, 0:16], T.tf[:, 0:16], T.pa[:, 0:1], A.mult, A.add, w=[t_pa])
    t_ct = scan(T.ct[:, 16:32], T.rl2[:, 16:32], T.tf[:, 16:32], T.pa[:, 1:2], A.mult, A.add)
    t_sx = scan(T.sx[:, 0:65], T.sd0[:, 0:65], T.x[:, 32:97], 0.0, A.mult, A.add, w=[t_x, t_sd, t_x1])
    t_co = tr(T.ce[:, 0:32], T.ct[:, :], w=[t_ct])
    t_r2 = act(T.r2[:, 0:1], T.ce[:, 31:32], None, 0.0, col(3), w=[t_co, t_c3])
    t_m1 = ts(T.m1[:, :], T.mb[:, :], pf(5), A.is_equal)
    t_code = cp(T.codel[:, :], T.ce[:, 0:32], w=[t_co])
    t_id = ts(T.id5[:, :], T.mi[:, 1:129], pf(0), A.is_equal, 520.0, A.mult)
    mm(T.pb[:, 0:1], T.m1[:, :], T.sx[:, 63:64], True, True, w=[t_sx, t_m1])
    mm(T.pd[:, 0:32], T.ml1[:, :], T.x[:, 32:64], True, False, w=[t_l])
    t_pd = mm(T.pd[:, 0:32], T.m1[:, :], T.sx[:, 0:32], False, True)
    t_pb = mm(T.pb[:, 1:3], T.m1[:, :], T.r2[:, 0:2], True, True, w=[t_r2])
    mm(T.pc[:, 0:33], T.ml1[:, :], T.x[:, 64:97], True, False, w=[t_x1])
    mm(T.pc[:, 0:33], T.m1[:, :], T.sx[:, 32:65], False, False)
    t_pc = mm(T.pc[:, 0:33], T.id5[:, :], T.ce[:, 0:33], False, True, w=[t_id, t_co, t_ext])

    others = [c for c in T.cores if c != core]

    def dst_id(c):
        rid, pid, _ = topo.addr(c)
        return DstId(rid=rid, pnc=pid)

    def common(src, dsts):
        m = topo.mask(src, dsts[0])
        for c in dsts:
            m &= topo.mask(src, c)
        return m

    t_vf = tt(T.vf[:, :], T.pd[:, 0:32], T.x[:, 0:32], A.min, w=[t_pd])
    t_exs = cp(T.exs[:, 0:3], T.pb[:, 0:3], w=[t_pb])
    use("g", t_exs)
    o = 4 * (q + 1)
    g.remote_dma_fused([RemoteDMATransfer(dst_ids=[dst_id(c) for c in others],
                                          dma_engine_mask=common(core, others), remote_sem=T.sem.exa,
                                          src=T.exs[:, 0:2], dsts=[T.ex[:, o:o + 2] for _ in others])],
                       local_sem=T.sem.exl)
    EXA = ("exa", sum(bin(common(c, [d for d in T.cores if d != c])).count("1") for c in others))
    i_ff = iota(T.ff[:, :], [[8, 8], [128, 4]], 1, 0)
    i_ti = iota(T.ti[:, :], [[1, 4], [512, 2], [0, 8]], 8 * q, 0)
    i_bs = iota(T.bsi[:, :], [[512, 2], [1, 4], [0, 2]], 0, 0)
    i_k8 = iota(T.k8[:, :], [[0, 8], [1, 8]], -8, 0)

    t_oh0 = act(T.oh[:, 0:256], T.cwin[:, 0:32].indirect(T.codel[:, 0:16]), w=[t_code, t_cw])
    t_oh1 = act(T.oh[:, 256:512], T.cwin[:, 0:32].indirect(T.codel[:, 16:32]))
    t_aa0 = act(T.aa[:, 0:256], T.cwin[:, 32:64].indirect(T.codel[:, 0:16]))
    t_aa1 = act(T.aa[:, 256:512], T.cwin[:, 32:64].indirect(T.codel[:, 16:32]))
    t_voff = ts(T.voffl[:, :], T.vf[:, :], 3.0, A.add, w=[t_vf])
    t_slot = ts(T.slotl[:, 0:33], T.pc[:, 0:33], T.exs[:, 2:3], A.subtract, 63.0, A.add, w=[t_pc, t_exs])

    vw = T.v[:, 0:516]
    t_b0 = tt(T.bb[:, 0:256], vw.indirect(T.voffl[:, 0:16]), T.oh[:, 0:256], A.add, w=[LDV, i_v, t_voff, t_oh0])
    t_b1 = tt(T.bb[:, 256:512], vw.indirect(T.voffl[:, 16:32]), T.oh[:, 256:512], A.add, w=[t_oh1])
    t = scan(T.sc[:, 1:257], T.aa[:, 0:256], T.bb[:, 0:256], -2.0, A.min, A.max, w=[t_b0, t_aa0, t_sc0])
    t = scan(T.sc[:, 257:513], T.aa[:, 256:512], T.bb[:, 256:512], T.sc[:, 256:257], A.min, A.max,
             w=[t_b1, t_aa1, t])
    t_scat = cp(T.win[:, 0:WIN].indirect(T.slotl[:, 0:33]), T.sc[:, :], w=[t, t_slot, t_sc0, t_w0, FIL])

    t_own = act(T.ex[:, o:o + 2], T.exs[:, 0:2], w=[t_exs])
    t_cb = act(col(8), col(7), None, -16.0 * NEG, -NEG)
    t_c9 = act(col(9), pf(3), None, pf(4), 64.0)
    act(T.cwin[:, 64:80], T.mi[:, 1:17], None, -64.0 * NEG, 0.0)
    t_w = act(T.cwin[:, 80:96], T.mi[:, 17:33], None, col(8), NEG, w=[t_cb])
    t_cst = act(T.cst[:, :], T.ff[:, :], None, col(9), w=[i_ff, t_c9])
    if q:
        t_kc = act(T.kc[:, :], T.cwin[:, 64:96].indirect(T.codel[:, 0:1]), w=[t_w])
    t = act(col(12), pf(2), None, 0.0, -28.0)
    act(col(11), pf(6), None, 0.0, 0.0625)
    t_c11 = act(col(10), pf(6), None, col(12), 32.0, w=[t])

    if q:
        t_nb = act(T.ctmp[:, 32:32 + q], T.ex[:, 4:4 + 4 * q:4], None, 0.0, -1.0, w=[EXA], accum=col(14))
        t_cm = act(T.cm[:, :], T.kc[:, :], ACT.Abs, T.ex[:, 4 * q + 1:4 * q + 2], -1.0, w=[t_kc])
        t_g1 = ts(T.g1[:, :], T.cst[:, :], col(14), A.add, T.exs[:, 2:3], A.subtract, w=[t_nb, t_cst])
        t_el = tt(T.el1[:, :], vw.indirect(T.voffl[:, 0:1]), T.cm[:, :], A.subtract, w=[t_cm])
        t_g2 = ts(T.g2[:, :], T.g1[:, :], NF - 1, A.bitwise_and, w=[t_g1])
        use("v", t_el)
        t = done("v", V.tensor_reduce(T.fixc[:, :], T.el1[:, :], AxisListType.X, A.max))
        t_gl = cp(T.gl[:, :], T.g2[:, :], w=[t_g2])
        t_fix = tt(T.win[:, 64:65], T.win[:, 64:65], T.fixc[:, :], A.max, w=[t, t_scat])
    else:
        t_g1 = ts(T.g1[:, :], T.cst[:, :], T.exs[:, 2:3], A.subtract, w=[t_cst])
        t_g2 = ts(T.g2[:, :], T.g1[:, :], NF - 1, A.bitwise_and, w=[t_g1])
        t_gl = cp(T.gl[:, :], T.g2[:, :], w=[t_g2])
        t_fix = t_scat
    t_f0 = cp(T.fr[:, 0:256], T.win[:, 64:576].indirect(T.gl[:, 0:16]), w=[t_gl, t_fix])
    t_f1 = act(T.fr[:, 256:512], T.win[:, 64:576].indirect(T.gl[:, 16:32]), w=[t_gl, t_fix])

    near = [d for d in range(8) if d != q and topo.die(T.cores[d]) == topo.die(core)]
    far = [d for d in range(8) if d != q and topo.die(T.cores[d]) != topo.die(core)]
    trs, k = [], 0
    while near or far:
        for h, side in enumerate((far, near)):
            if not side:
                continue
            d = side.pop(0)
            e = topo.engines(core, T.cores[d])
            trs.append(RemoteDMATransfer(dst_ids=[dst_id(T.cores[d])],
                                         dma_engine_mask=(1 << e[k + h]) | (1 << e[k + 2 + h]),
                                         remote_sem=T.sem.ma, src=T.fr[:, SLOTS * d:SLOTS * d + SLOTS],
                                         dst=T.land[:, SLOTS * q:SLOTS * q + SLOTS]))
        k += 4
    use("g", t_f0, t_f1)
    g.remote_dma_fused(trs, local_sem=T.sem.ml)
    i_ls = iota(T.land[:, NF:NF + 64], [[0, 64]], -2, 0)
    i_pm = iota(T.pmi[:, :], [[16, 2], [32, 4]], 0, 0)

    t_q1 = act(T.tq1[:, :], T.ti[:, :], None, col(10), w=[t_c11, i_ti])
    t_q0 = act(T.tq[:, :], T.tq1[:, :], None, -0.5, w=[t_q1])
    t_bs = act(T.bs[:, :], T.bsi[:, :], None, col(11), 0.015625, w=[i_bs])
    t_me = act(T.land[:, SLOTS * q:SLOTS * q + SLOTS], T.fr[:, SLOTS * q:SLOTS * q + SLOTS], w=[t_f0, t_f1])
    t_xa = scan(T.xa[:, 1:8], T.ex[:, 4:32:4], T.zr[:, 0:7], -1.0, A.add, A.add, w=[EXA, t_own, t_zr])
    t_xb = ts(T.xb[:, 1:8], T.ex[:, 8:36:4], 512.0, A.is_ge, 0.25, A.mult)
    ts(T.xe[:, 0:1], T.xa[:, 7:8], T.ex[:, 32:33], A.add, 0.25, A.add, w=[t_xa, EXA])
    t_el = ts(T.elist[:, :], T.zr[:, 0:4], pf(4), A.add)
    t_xe = tt(T.xe[:, 1:8], T.xa[:, 1:8], T.xb[:, 1:8], A.add, w=[t_xb])
    t_te = cp(T.te[:, :], T.xe[:, 0:8].indirect(T.elist[:, 0:4]), w=[t_xe, t_el])
    t_eq = tt(T.eq[:, :], T.tq1[:, :], T.te[:, :], A.is_equal, w=[t_te, t_q1])
    t2 = tt(T.pq[:, 0:64], T.tq[:, :], T.te[:, :], A.is_ge, w=[t_q0])
    t = tt(T.pq[:, 64:128], T.eq[:, :], T.k8[:, :], A.mult, w=[t_eq, i_k8])
    t = scan(T.cum[:, 1:129], T.pq[:, :], T.zr[:, 0:128], 0.0, A.add, A.add, w=[t, t2, t_cum])
    t = tt(T.dif[:, :], T.cum[:, 8:129:8], T.cum[:, 0:128:8], A.subtract, w=[t])
    t = tt(T.off[:, :], T.dif[:, :], T.bs[:, :], A.add, w=[t, t_bs])
    t_lst = ts(T.lst[:, :], T.off[:, :], float(SLOTS), A.mult, w=[t])
    t_prm = ts(T.prm[:, :], T.pmi[:, :], pf(6), A.add, w=[i_pm])

    MA = ("ma", 14)
    land = T.land[:, 0:NF + 64]
    t_a = act(T.sec[:, 0:64], land.indirect(T.lst[:, 8:12]), w=[t_lst, i_ls, t_me, MA])
    t_b = act(T.sec[:, 64:128], land.indirect(T.lst[:, 12:16]))
    t_a = tt(T.ym[:, 0:64], land.indirect(T.lst[:, 0:4]), T.sec[:, 0:64], A.max, w=[MA, t_lst, i_ls, t_me, t_a])
    t_b = tt(T.ym[:, 64:128], land.indirect(T.lst[:, 4:8]), T.sec[:, 64:128], A.max, w=[t_b])
    tr(T.zt[:, 0:64], T.ym[:, 0:64], w=[t_a])
    t_zt = tr(T.zt[:, 64:128], T.ym[:, 64:128], w=[t_b])
    t_z0 = cp(T.zf0[:, :], T.zt[:, :].indirect(T.prm[:, 0:4]), w=[t_zt, t_prm])
    t_z1 = act(T.zf1[:, :], T.zt[:, :].indirect(T.prm[:, 4:8]), w=[t_zt, t_prm])
    use("y", t_z0)
    g.sync.dma_start(T.y[0::2, :], T.zf0[:, :]).then_inc(T.sem.st, 16)
    use("s", t_z1)
    S.dma_start(T.y[1::2, :], T.zf1[:, :]).then_inc(T.sem.st, 16)

    use("y", ("st", 32))
    for k in ("v", "s", "p", "g"):
        use("g", ("c" + k, cnt[k]))
    use("g", ("exl", bin(common(core, others)).count("1")), ("ml", 14), EXA, FIL, LDR, LDD, LDV)
